import numpy as np
import ml_dtypes


def mxq(x, axis, fmt="e4m3"):
    dtype, down = {"e4m3": (ml_dtypes.float8_e4m3fn, 7), "e5m2": (ml_dtypes.float8_e5m2, 14)}[fmt]
    v = np.moveaxis(np.asarray(x, np.float32).astype(ml_dtypes.bfloat16).astype(np.float64), axis, -1)
    blocks = v.reshape(v.shape[:-1] + (-1, 32))
    amax = np.abs(blocks).max(-1, keepdims=True)
    byte = np.maximum(np.where(amax > 0, np.frexp(amax)[1] - 1 + 127, 0) - down, 1)
    scale = np.exp2(byte - 127.0)
    codes = (blocks / scale).astype(np.float32).astype(dtype).astype(np.float64)
    return np.moveaxis((codes * scale).reshape(v.shape), -1, axis)


WIDE = False


def mx_kscale(k):
    if not WIDE:
        return np.ones(k)
    levels = np.array([10, -10, 5, -5, 0])
    if k % 512:
        return np.exp2(np.random.permutation(np.resize(levels, k // 32))).repeat(32)
    a = np.empty((k // 512, 16))
    for p in range(k // 512):
        a[p, :8] = np.random.permutation(np.resize(levels, 8))
        for g in range(8):
            far = levels[np.abs(levels - a[p, g]) >= 10]
            a[p, g + 8] = far[np.random.randint(len(far))]
    return np.exp2(a.ravel()).repeat(32)


def f64(x):
    return np.asarray(x).astype(np.float64)


def striped(idx):
    return np.tile(idx.reshape(-1, 16).T, (8, 1)).astype(np.uint16)


def unstriped(offs):
    return offs[:16].T.reshape(-1).astype(np.int64)


E2M1 = np.array([0.0, 0.5, 1.0, 1.5, 2.0, 3.0, 4.0, 6.0, -0.0, -0.5, -1.0, -1.5, -2.0, -3.0, -4.0, -6.0])


def pack_weight(w, fmt):
    k, n = w.shape
    w = f64(np.asarray(w, np.float32).astype(ml_dtypes.bfloat16)).reshape(k // 32, 32, n)
    amax = np.abs(w).max(1)
    if fmt == "e4m3":
        byte = np.frexp(amax)[1] - 1 + 127 - 7
    else:
        mant, ex = np.frexp(amax / 6.0)
        byte = np.where(mant > 0.5, ex, ex - 1) + 127
    byte = np.clip(np.where(amax > 0, byte, 1), 1, 254)
    scaled = (w * np.exp2(127.0 - byte)[:, None, :]).reshape(k, n).astype(np.float32)
    by_word = np.ascontiguousarray(scaled.reshape(k // 512, 128, 4, n).transpose(0, 1, 3, 2))
    if fmt == "e4m3":
        words = by_word.astype(ml_dtypes.float8_e4m3fn).view(np.uint8)
    else:
        c = by_word.astype(ml_dtypes.float4_e2m1fn).view(np.uint8) & 0xF
        words = (c[..., 0::2] | (c[..., 1::2] << 4)).reshape(k // 512, 128, 2 * n)
    return np.ascontiguousarray(words), np.ascontiguousarray(byte.astype(np.uint8).reshape(k // 512, 16, n))


def unpack_weight(words, scales, fmt):
    g, _, n = scales.shape
    words = np.ascontiguousarray(words).reshape(g, 128, n, -1)
    if fmt == "e4m3":
        vals = words.view(ml_dtypes.float8_e4m3fn).astype(np.float64)
    else:
        nib = np.empty((g, 128, n, 4), np.uint8)
        nib[..., 0::2] = words & 0xF
        nib[..., 1::2] = words >> 4
        vals = E2M1[nib]
    vals = vals * np.repeat(np.exp2(scales.astype(np.float64) - 127.0), 8, axis=1)[..., None]
    return vals.transpose(0, 1, 3, 2).reshape(g * 512, n)


def gelu(v):
    return 0.5 * v * (1.0 + np.tanh(np.sqrt(2.0 / np.pi) * (v + 0.044715 * v**3)))


K, H, N, T, S, P, T2 = 1024, 1536, 768, 2048, 512, 512, 1024

def setup_inputs():
    n = np.random.standard_normal
    s = mx_kscale(K)[:, None]
    u = mx_kscale(H)[:, None]
    d = {}
    d["tab_words"], d["tab_scales"] = pack_weight(n((K, T)) * s, "e4m3")
    d["offs"] = striped(np.random.permutation(T)[:S])
    d["w1"] = (1.5 * n((K, H)) / K**0.5 / s).astype(np.float32)
    d["gain"] = (1.2 * np.exp(0.3 * n(H)) * u[:, 0]).astype(np.float32)
    d["page0"] = (n((H, T2)) * u).astype(np.float32)
    d["offs2"] = striped(np.random.permutation(T2)[:S])
    d["wgs"] = np.exp(0.3 * n((128, S))).astype(np.float32)
    d["offs3"] = striped(np.random.permutation(T2)[:P])
    d["trial"] = (0.8 * n((H, P)) * u).astype(np.float32)
    d["w2_words"], d["w2_scales"] = pack_weight(n((H, N)) / H**0.5 / u, "e2m1")
    d["w3_words"], d["w3_scales"] = pack_weight(n((K, N)) / K**0.5 / s, "e4m3")
    d["w4"] = (0.6 * n((H, N)) / H**0.5 / u).astype(np.float32)
    d["page1"] = n((N, T2)).astype(np.float32)
    d["offs4"] = striped(np.random.permutation(T2)[:P])
    d["wgo"] = np.exp(0.3 * n((128, P))).astype(np.float32)
    return d

def reference(tab_words, tab_scales, offs, w1, gain, page0, offs2, wgs, offs3, trial, w2_words, w2_scales, w3_words, w3_scales, w4, page1, offs4, wgo):
    v = unpack_weight(tab_words, tab_scales, "e4m3")[:, unstriped(offs)]
    p1 = mxq(f64(w1), 0, "e4m3").T @ v
    h = f64(gain)[:, None] * (p1 / (1.0 + np.exp(-p1)))
    page = f64(page0).copy()
    page[:, unstriped(offs2)] = np.tile(f64(wgs), (H // 128, 1)) * h
    x = page[:, unstriped(offs3)] + f64(trial)
    xq = mxq(x, 0, "e4m3")
    p2 = unpack_weight(w2_words, w2_scales, "e2m1").T @ xq + unpack_weight(w3_words, w3_scales, "e4m3").T @ v
    y = np.tanh(p2) + (mxq(f64(w4), 0, "e4m3").T @ xq)
    out = f64(page1).copy()
    out[:, unstriped(offs4)] = np.tile(f64(wgo), (N // 128, 1)) * y
    return out

@@ -1,0 +1,381 @@
+from contextlib import ExitStack
+
+import concourse.mybir as mybir
+from concourse.masks import make_identity
+
+K, H, N, T, S, T2 = 1024, 1536, 768, 2048, 512, 1024
+FLOPS = 2 * S * (K * H + H * N + K * N + H * N)
+
+F32 = mybir.dt.float32
+BF16 = mybir.dt.bfloat16
+I32 = mybir.dt.int32
+U32 = mybir.dt.uint32
+U16 = mybir.dt.uint16
+U8 = mybir.dt.uint8
+FP8X4 = mybir.dt.float8_e4m3fn_x4
+FP4X4 = mybir.dt.float4_e2m1fn_x4
+ACT = mybir.ActivationFunctionType
+MULT = mybir.AluOpType.mult
+
+P = 128
+KP = 512
+KA, HA = K // KP, H // KP
+SLICES = H // P
+NT = N // P
+JT = S // P
+HALF = S // 2
+BULK = {
+    1: (("w1", 3, 2),),
+    2: (("w1", 5, 2),),
+    3: (("w4", 0, 0, 256), ("w4", 1, 0, 256)),
+    4: (("w1", 7, 2),),
+    5: (("w4", 0, 256, 512),),
+    6: (("w1", 9, 2),),
+    7: (("w1", 11, 1), ("w4", 2, 0, 256)),
+    8: (("w4", 1, 256, 512),),
+    10: (("w4", 2, 256, 512),),
+}
+AFTER_TRIAL = {1: "w1w_5", 3: "w1w_7", 4: "x_0", 5: "w1w_9", 6: "w4_first", 7: "w1w_11", 8: "x_1"}
+
+
+def tile_list_mattress_sag_page_kernel(
+    tc, tab_words, tab_scales, offs, w1, gain, page0, offs2, wgs, offs3, trial,
+    w2_words, w2_scales, w3_words, w3_scales, w4, page1, offs4, wgo, out,
+):
+    nc = tc.nc
+    with ExitStack() as ctx:
+        lists = ctx.enter_context(tc.tile_pool(name="lists", bufs=1))
+        keep = ctx.enter_context(tc.tile_pool(name="keep", bufs=1))
+        ring = ctx.enter_context(tc.tile_pool(name="ring", bufs=2))
+        psum = ctx.enter_context(tc.psum_pool(name="psum", bufs=2))
+
+        def load_list(src, name):
+            t = lists.tile([P, S // 16], U16, name=name)
+            nc.sync.dma_start(t[:], src)
+            return t
+
+        idx = load_list(offs, "idx")
+        tab_s = keep.tile([P, T], U8, name="tab_s", align_bytes=64)
+        nc.gpsimd.memset(tab_s[:].bitcast(I32), 0)
+        gain_rows = keep.tile([P, P], F32, name="gain_rows")
+        nc.vector.memset(gain_rows[:], 0.0)
+        warm = keep.tile([P, 1], F32, name="warm")
+        nc.scalar.activation(warm[:], gain_rows[:, P - 1 : P], ACT.Silu)
+        v_w = []
+        v_s = keep.tile([P, S], U8, name="v_s", align_bytes=64)
+        for a in range(KA):
+            tw = ring.tile([P, T], U32, name="tw", tag="raw", bufs=4, align_bytes=64)
+            nc.sync.dma_start(
+                tw[:].bitcast(I32), tab_words[a].rearrange("p t i -> p (t i)").bitcast(I32)
+            )
+            vw = keep.tile([P, S], U32, name="v_w%d" % a, align_bytes=64)
+            nc.vector.tensor_copy(vw[:], tw[:].indirect(idx[:]))
+            v_w.append(vw)
+            if a == 0:
+                for q in range(4):
+                    nc.sync.dma_start(
+                        tab_s[32 * q : 32 * q + 8, :].bitcast(I32),
+                        tab_scales[:, 4 * q : 4 * q + 4, :].bitcast(I32),
+                    )
+                nc.sync.dma_start(gain_rows[0:SLICES, :], gain.rearrange("(s q) -> s q", q=P))
+                nc.vector.tensor_copy(v_s[:], tab_s[:].indirect(idx[:]))
+
+        ident = keep.tile([P, P], F32, name="ident")
+        make_identity(nc, ident[:])
+        w2_s = keep.tile([P, HA, N], U8, name="w2_s", align_bytes=64)
+        w3_s = keep.tile([P, KA, N], U8, name="w3_s", align_bytes=64)
+        nc.gpsimd.memset(w2_s[:].rearrange("p a c -> p (a c)").bitcast(I32), 0)
+        nc.gpsimd.memset(w3_s[:].rearrange("p a c -> p (a c)").bitcast(I32), 0)
+
+        banks = [psum.tile([P, S], F32, name="bank%d" % i, bufs=1) for i in range(2)]
+        gain_ps = psum.tile([P, P], F32, name="gain_ps", tag="tr")
+        nc.tensor.transpose(gain_ps[:], gain_rows[:], ident[:])
+        gain_sb = keep.tile([P, SLICES], F32, name="gain_sb")
+        nc.scalar.copy(gain_sb[:], gain_ps[:, 0:SLICES])
+
+        def round_rows(dst, rows):
+            nc.scalar.copy(
+                dst.rearrange("p (c e i) -> p c i e", e=4, i=4),
+                rows.rearrange("p i (c e) -> p c i e", e=4),
+            )
+
+        def quantize(codes, scales, g):
+            nc.vector.quantize_mx(codes.bitcast(FP8X4), scales, g)
+
+        w1_q = {}
+        w4_g = keep.tile([P, HA, 4 * N], BF16, name="w4g", align_bytes=64)
+        w4_s = keep.tile([P, HA, N], U8, name="w4s", align_bytes=64)
+        waiting = {}
+        w4_w = []
+
+        def quantize_w4_first():
+            codes = keep.tile([P, HA, 256], U32, name="w4_first", align_bytes=64)
+            for b in range(HA):
+                quantize(codes[:, b, :], w4_s[:, b, 0:256], w4_g[:, b, 0:1024])
+            w4_w.append(codes[:])
+
+        waiting["w4_first"] = quantize_w4_first
+
+        def load_rows(dst, src, a, c0, width):
+            rows = dst.rearrange("p (i c) -> p i c", i=4)
+            nc.sync.dma_start(
+                rows, src[KP * a : KP * (a + 1), c0 : c0 + width].rearrange("(p i) c -> p i c", i=4)
+            )
+            return rows
+
+        def load_bulk(items, tag="raw", bufs=4):
+            size = sum(8 * P * it[2] if it[0] == "w1" else 4 * it[3] for it in items)
+            raw = ring.tile([P, size], F32, name="raw", tag=tag, bufs=bufs, align_bytes=64)
+            loaded = []
+            at = 0
+            for it in items:
+                if it[0] == "w1":
+                    width = P * it[2]
+                    rows = [load_rows(raw[:, at + 4 * width * a : at + 4 * width * (a + 1)], w1, a, P * it[1], width)
+                            for a in range(KA)]
+                    at = at + 8 * width
+                else:
+                    rows = load_rows(raw[:, at : at + 4 * it[3]], w4, it[1], it[2], it[3])
+                    at = at + 4 * it[3]
+                loaded.append((it, rows))
+            return loaded
+
+        def prepare_w1(s0, count, rows):
+            width = P * count
+            g = ring.tile([P, KA, 4 * width], BF16, name="w1g", tag="first" if s0 == 1 else "w1g",
+                          bufs=1 if s0 == 1 else 2, align_bytes=64)
+            for a in range(KA):
+                round_rows(g[:, a, :], rows[a])
+
+            def finish():
+                codes = keep.tile([P, KA, width], U32, name="w1w_%d" % s0, align_bytes=64)
+                scales = keep.tile([P, KA, width], U8, name="w1s_%d" % s0, align_bytes=64)
+                quantize(
+                    codes[:].rearrange("p a c -> p (a c)"), scales[:].rearrange("p a c -> p (a c)"),
+                    g[:].rearrange("p a c -> p (a c)"),
+                )
+                for a in range(KA):
+                    for i in range(count):
+                        cs = slice(P * i, P * (i + 1))
+                        w1_q[(a, s0 + i)] = (codes[:, a, cs], scales[:, a, cs])
+
+            if s0 < 5:
+                finish()
+            else:
+                waiting["w1w_%d" % s0] = finish
+
+        def prepare(loaded):
+            for it, rows in loaded:
+                if it[0] == "w1":
+                    prepare_w1(it[1], it[2], rows)
+                else:
+                    b, c0, width = it[1:]
+                    for c in range(0, width, 256):
+                        round_rows(w4_g[:, b, 4 * (c0 + c) : 4 * (c0 + c + 256)], rows[:, :, c : c + 256])
+
+        pages = {}
+
+        def put_slice(s):
+            p1 = banks[s % 2]
+            last = s == SLICES - 1
+            wg = ring.tile([P, S], F32, name="wg", tag="wg", bufs=SLICES - 1)
+            nc.scalar.activation(wg[:], wgs_sb[:], ACT.Copy, scale=gain_sb[:, s : s + 1])
+            for a in range(KA):
+                codes, scales = w1_q[(a, s)]
+                nc.tensor.matmul_mx(
+                    p1[:], lhsT=codes.bitcast(FP8X4), lhsT_scale=scales,
+                    rhs=v_w[a][:].bitcast(FP8X4), rhs_scale=v_s[4 * a : P, :],
+                    start=(a == 0), stop=(a == KA - 1),
+                )
+            h = ring.tile([P, S], F32, name="h", tag="late_h" if last else "h", bufs=1 if last else 2)
+            nc.scalar.activation(h[:], p1[:], ACT.Silu)
+            page = ring.tile([P, T2], F32, name="page", tag="page", bufs=5)
+            nc.sync.dma_start(page[:], page0[P * s : P * (s + 1), :])
+            nc.vector.tensor_tensor(page[:].indirect(idx2[:]), h[:], wg[:], MULT)
+            pages[s] = page
+
+        x_t = {}
+        x_w = {}
+        x_s = keep.tile([P, HA, S], U8, name="x_s", align_bytes=64)
+
+        def fetch(s, dst, j0, count):
+            nc.vector.tensor_copy(dst, pages[s][:].indirect(idx3[:, j0 // 16 : (j0 + count) // 16]))
+
+        def turn(s, src, j0, count, bank):
+            b, sl = divmod(s, 4)
+            if j0 == 0 and s in AFTER_TRIAL:
+                given = keep.tile([P, count], F32, name="given", tag=AFTER_TRIAL[s], align_bytes=64)
+            elif j0 == 0:
+                given = ring.tile([P, count], F32, name="given", tag="trial", bufs=3)
+            else:
+                given = ring.tile([P, count], F32, name="given", tag="trial_rest", bufs=4)
+            nc.sync.dma_start(given[:], trial[P * s : P * (s + 1), j0 : j0 + count])
+            for c in range(0, count, P):
+                nc.tensor.matmul(bank[:, c : c + P], given[:, c : c + P], ident[:],
+                                 start=(c == 0), stop=False, is_transpose=True)
+            for c in range(0, count, P):
+                nc.tensor.matmul(bank[:, c : c + P], src[:, c : c + P], ident[:],
+                                 start=False, stop=(c == count - P), is_transpose=True)
+            if b not in x_t:
+                x_t[b] = ring.tile([P, JT, 2, P, 2], BF16, name="xt", tag="xt", bufs=2)
+            nc.scalar.copy(
+                x_t[b][:, j0 // P : (j0 + count) // P, :, 32 * sl : 32 * (sl + 1), :],
+                bank[:, 0:count].rearrange("j (t p u e) -> j t u p e", p=32, u=2, e=2),
+            )
+
+        def turn_back(b, half, xi):
+            words = x_t[b][:].rearrange("j t u p e -> j (t u p e)").bitcast(F32)
+            back = psum.tile([P, 2, 2, P], F32, name="back", tag="tr")
+            for t in range(2):
+                for u in range(2):
+                    w0 = P * (2 * (2 * half + t) + u)
+                    nc.tensor.transpose(back[:, t, u, :], words[:, w0 : w0 + P], ident[:])
+            nc.scalar.copy(
+                xi.rearrange("p (t j u) -> p t j u", t=2, u=2), back[:].rearrange("p t u j -> p t j u")
+            )
+
+        def finish_block(b):
+            xi = ring.tile([P, 2, S], F32, name="xi", tag="xi", bufs=1, align_bytes=64)
+            for half in range(2):
+                turn_back(b, half, xi[:, half, :])
+
+            def finish():
+                x_w[b] = keep.tile([P, S], U32, name="x_%d" % b, align_bytes=64)
+                quantize(x_w[b][:], x_s[:, b, :], xi[:].rearrange("p h w -> p (h w)").bitcast(BF16))
+
+            waiting["x_%d" % b] = finish
+
+        def finish_half(b, half):
+            xi = ring.tile([P, S], F32, name="xih", tag="later" if half == 0 else "xih", bufs=1, align_bytes=64)
+            turn_back(b, half, xi[:])
+            js = slice(HALF * half, HALF * (half + 1))
+            if half == 0:
+                x_w[b] = keep.tile([P, S], U32, name="x_%d" % b, align_bytes=64)
+            quantize(x_w[b][:, js], x_s[:, b, js], xi[:].bitcast(BF16))
+
+        prepare(load_bulk((("w1", 0, 1),), "bounded", 2))
+        wgs_sb = keep.tile([P, S], F32, name="wgs_sb")
+        nc.sync.dma_start(wgs_sb[:], wgs)
+        idx2 = load_list(offs2, "idx2")
+        idx3 = load_list(offs3, "idx3")
+        w2_w = keep.tile([P, HA, 2 * N], U8, name="w2_w", align_bytes=64)
+        w3_w = keep.tile([P, KA, N], U32, name="w3_w", align_bytes=64)
+        ahead = {}
+        SPLIT = SLICES - 4
+        for s in range(SLICES + 2):
+            if s < SLICES:
+                put_slice(s)
+            if s == 0:
+                prepare(load_bulk((("w1", 1, 2),)))
+                got = ring.tile([P, S], F32, name="got", tag="first", bufs=1, align_bytes=64)
+            if s >= 2:
+                width = S if s - 2 < SPLIT else HALF
+                g0 = HALF if s - 2 == SLICES - 2 else 0
+                turn(s - 2, got[:, g0 : g0 + width], 0, width, banks[s % 2])
+            if 1 <= s <= SLICES:
+                width = S if s - 1 < SPLIT else HALF
+                g0 = HALF if s - 1 == SLICES - 2 else 0
+                fetch(s - 1, got[:, g0 : g0 + width], 0, width)
+            if s - 2 in AFTER_TRIAL:
+                waiting[AFTER_TRIAL[s - 2]]()
+            for w in (() if s == 0 else (1, 2) if s == 1 else (3, 4) if s == 2 else (s + 2,)):
+                if w in BULK:
+                    ahead[w] = load_bulk(BULK[w])
+            if s in BULK:
+                prepare(ahead[s])
+            if s == 9:
+                for q in range(4):
+                    nc.sync.dma_start(
+                        w2_s[32 * q : 32 * q + 4, :, :].bitcast(I32),
+                        w2_scales[:, 4 * q : 4 * q + 4, :].rearrange("a r c -> r a c").bitcast(I32),
+                    )
+                    nc.sync.dma_start(
+                        w3_s[32 * q : 32 * q + 4, :, :].bitcast(I32),
+                        w3_scales[:, 4 * q : 4 * q + 4, :].rearrange("a r c -> r a c").bitcast(I32),
+                    )
+            if s == 8:
+                nc.sync.dma_start(
+                    w2_w[:].bitcast(I32), w2_words.rearrange("a p c -> p a c").bitcast(I32)
+                )
+            if s == 7:
+                nc.sync.dma_start(
+                    w3_w[:].bitcast(I32),
+                    w3_words.rearrange("a p c i -> p a (c i)").bitcast(I32),
+                )
+            if s in (5, 9):
+                finish_block((s - 5) // 4)
+        finish_half(HA - 1, 0)
+        rest = ring.tile([P, 4, HALF], F32, name="rest", tag="late_h", bufs=1)
+        for s in range(SPLIT, SLICES):
+            fetch(s, rest[:, s - SPLIT, :], HALF, HALF)
+            turn(s, rest[:, s - SPLIT, :], HALF, HALF, banks[s % 2])
+        w4_rest = ring.tile([P, HA, 512], U32, name="w4_rest", tag="later", bufs=1, align_bytes=64)
+        for b in range(HA):
+            quantize(w4_rest[:, b, :], w4_s[:, b, 256:N], w4_g[:, b, 1024 : 4 * N])
+        w4_w.extend((w4_rest[:, :, 0:256], w4_rest[:, :, 256:512]))
+
+        idx4 = load_list(offs4, "idx4")
+        wgo_sb = keep.tile([P, S], F32, name="wgo_sb")
+        nc.sync.dma_start(wgo_sb[:], wgo)
+        out_pages = []
+        for n in range(NT):
+            page = keep.tile([P, T2], F32, name="out_page%d" % n)
+            nc.sync.dma_start(page[:], page1[P * n : P * (n + 1), :])
+            out_pages.append(page)
+        for pair in range(NT // 2):
+            c0 = 2 * P * pair
+            cols = slice(c0, c0 + 2 * P)
+            for half in range(2):
+                if pair == 0 and half == 1:
+                    finish_half(HA - 1, 1)
+                p2 = psum.tile([P, 2, 2 * P], F32, name="p2", tag="y", bufs=4)
+                p4 = psum.tile([P, 2, 2 * P], F32, name="p4", tag="y", bufs=4)
+                tiles = [slice(HALF * half + P * t, HALF * half + P * (t + 1)) for t in range(2)]
+                for a in range(KA):
+                    for t, js in enumerate(tiles):
+                        nc.tensor.matmul_mx(
+                            p2[:, t, :], lhsT=v_w[a][:, js].bitcast(FP8X4), lhsT_scale=v_s[4 * a : P, js],
+                            rhs=w3_w[:, a, cols].bitcast(FP8X4), rhs_scale=w3_s[:, a, cols],
+                            start=(a == 0 and t == 0), stop=False,
+                        )
+                for b in range(HA):
+                    for t, js in enumerate(tiles):
+                        for i in range(2):
+                            n0 = c0 + P * i
+                            nc.tensor.matmul_mx(
+                                p2[:, t, P * i : P * (i + 1)],
+                                lhsT=x_w[b][:, js].bitcast(FP8X4), lhsT_scale=x_s[:, b, js],
+                                rhs=w2_w[:, b, 2 * n0 : 2 * (n0 + P)].bitcast(FP4X4),
+                                rhs_scale=w2_s[:, b, n0 : n0 + P],
+                                start=False, stop=(b == HA - 1 and t == 1 and i == 1),
+                            )
+                    for t, js in enumerate(tiles):
+                        nc.tensor.matmul_mx(
+                            p4[:, t, :], lhsT=x_w[b][:, js].bitcast(FP8X4), lhsT_scale=x_s[:, b, js],
+                            rhs=w4_w[pair][:, b, :].bitcast(FP8X4), rhs_scale=w4_s[:, b, cols],
+                            start=(b == 0 and t == 0), stop=(b == HA - 1 and t == 1),
+                        )
+                bounded = ring.tile([P, 2, 2 * P], F32, name="bounded", tag="bounded", align_bytes=64)
+                nc.scalar.activation(bounded[:], p2[:], ACT.Tanh)
+                bare = ring.tile([P, 2, 2 * P], F32, name="bare", tag="bare")
+                if pair == 0 and half == 0:
+                    nc.vector.tensor_copy(bare[:], p4[:])
+                else:
+                    nc.scalar.copy(bare[:], p4[:])
+                y_ps = psum.tile([P, 2, 2, P], F32, name="y_ps", tag="tr")
+                for i in range(2):
+                    for t in range(2):
+                        ns = slice(P * i, P * (i + 1))
+                        nc.tensor.matmul(y_ps[:, i, t, :], bounded[:, t, ns], ident[:],
+                                         start=True, stop=False, is_transpose=True)
+                        nc.tensor.matmul(y_ps[:, i, t, :], bare[:, t, ns], ident[:],
+                                         start=False, stop=True, is_transpose=True)
+                y = ring.tile([P, 2, HALF], F32, name="y", tag="y_sb")
+                nc.scalar.copy(y[:], y_ps[:].rearrange("p i t j -> p i (t j)"))
+                js = slice(HALF * half, HALF * (half + 1))
+                entries = idx4[:, HALF * half // 16 : HALF * (half + 1) // 16]
+                for i in range(2):
+                    n = 2 * pair + i
+                    nc.vector.tensor_tensor(out_pages[n][:].indirect(entries), y[:, i, :], wgo_sb[:, js], MULT)
+                    if half == 1:
+                        nc.sync.dma_start(out[P * n : P * (n + 1), :], out_pages[n][:])

@@ -16,6 +16,7 @@ FP8X4 = mybir.dt.float8_e4m3fn_x4
 FP4X4 = mybir.dt.float4_e2m1fn_x4
 ACT = mybir.ActivationFunctionType
 MULT = mybir.AluOpType.mult
+ADD = mybir.AluOpType.add
 
 P = 128
 KP = 512
@@ -24,18 +25,23 @@ SLICES = H // P
 NT = N // P
 JT = S // P
 HALF = S // 2
+UNITS = ((0, 0), (1, 0), (0, 1), (1, 1), (2, 0), (2, 1))
 BULK = {
     1: (("w1", 3, 2),),
     2: (("w1", 5, 2),),
-    3: (("w4", 0, 0, 256), ("w4", 1, 0, 256)),
-    4: (("w1", 7, 2),),
-    5: (("w4", 0, 256, 512),),
-    6: (("w1", 9, 2),),
-    7: (("w1", 11, 1), ("w4", 2, 0, 256)),
+    3: (("w1", 7, 1), ("w4", 0, 0, 256)),
+    4: (("dealt", 0),),
+    5: (("dealt", 1),),
+    6: (("w4", 1, 0, 256), ("w4", 2, 0, 256)),
+    7: (("w4", 0, 256, 512),),
     8: (("w4", 1, 256, 512),),
     10: (("w4", 2, 256, 512),),
 }
-AFTER_TRIAL = {1: "w1w_5", 3: "w1w_7", 4: "x_0", 5: "w1w_9", 6: "w4_first", 7: "w1w_11", 8: "x_1"}
+AFTER_TRIAL = {1: "w1w_5", 3: "w1w_7", 4: "w1w_8", 5: "x_0", 6: "w4_first"}
+SPLIT = SLICES - 4
+LAST_FETCH = {9: (8,), 10: (9, 10), 11: (11,)}
+LOADS = {0: (), 1: (1, 2), 2: (3,), 3: (4, 5)}
+H_TAGS = {SLICES - 2: "x_1", SLICES - 1: "late_h"}
 
 
 def tile_list_mattress_sag_page_kernel(
@@ -77,7 +83,7 @@ def tile_list_mattress_sag_page_kernel(
                         tab_s[32 * q : 32 * q + 8, :].bitcast(I32),
                         tab_scales[:, 4 * q : 4 * q + 4, :].bitcast(I32),
                     )
-                nc.sync.dma_start(gain_rows[0:SLICES, :], gain.rearrange("(s q) -> s q", q=P))
+                nc.sync.dma_start(gain_rows[0:SPLIT, :], gain[0 : P * SPLIT].rearrange("(s q) -> s q", q=P))
                 nc.vector.tensor_copy(v_s[:], tab_s[:].indirect(idx[:]))
 
         ident = keep.tile([P, P], F32, name="ident")
@@ -88,10 +94,10 @@ def tile_list_mattress_sag_page_kernel(
         nc.gpsimd.memset(w3_s[:].rearrange("p a c -> p (a c)").bitcast(I32), 0)
 
         banks = [psum.tile([P, S], F32, name="bank%d" % i, bufs=1) for i in range(2)]
-        gain_ps = psum.tile([P, P], F32, name="gain_ps", tag="tr")
+        gain_ps = psum.tile([P, P], F32, name="gain_ps", tag="tr", bufs=1)
         nc.tensor.transpose(gain_ps[:], gain_rows[:], ident[:])
-        gain_sb = keep.tile([P, SLICES], F32, name="gain_sb")
-        nc.scalar.copy(gain_sb[:], gain_ps[:, 0:SLICES])
+        gain_sb = keep.tile([P, SPLIT], F32, name="gain_sb")
+        nc.scalar.copy(gain_sb[:], gain_ps[:, 0:SPLIT])
 
         def round_rows(dst, rows):
             nc.scalar.copy(
@@ -124,7 +130,7 @@ def tile_list_mattress_sag_page_kernel(
             return rows
 
         def load_bulk(items, tag="raw", bufs=4):
-            size = sum(8 * P * it[2] if it[0] == "w1" else 4 * it[3] for it in items)
+            size = sum(8 * P * it[2] if it[0] == "w1" else 4 * KP if it[0] == "dealt" else 4 * it[3] for it in items)
             raw = ring.tile([P, size], F32, name="raw", tag=tag, bufs=bufs, align_bytes=64)
             loaded = []
             at = 0
@@ -134,6 +140,8 @@ def tile_list_mattress_sag_page_kernel(
                     rows = [load_rows(raw[:, at + 4 * width * a : at + 4 * width * (a + 1)], w1, a, P * it[1], width)
                             for a in range(KA)]
                     at = at + 8 * width
+                elif it[0] == "dealt":
+                    rows = load_rows(raw[:], w1, it[1], P * SPLIT, KP)
                 else:
                     rows = load_rows(raw[:, at : at + 4 * it[3]], w4, it[1], it[2], it[3])
                     at = at + 4 * it[3]
@@ -164,22 +172,59 @@ def tile_list_mattress_sag_page_kernel(
             else:
                 waiting["w1w_%d" % s0] = finish
 
+        dealt = {}
+
+        def deal_w1(a, rows):
+            dealt[a] = ring.tile([P, 4 * KP], BF16, name="w1g", tag="w1g", bufs=2, align_bytes=64)
+            nc.scalar.copy(
+                dealt[a][:].rearrange("p (t m i) -> p m i t", t=4, i=4),
+                rows.rearrange("p i (m t) -> p m i t", t=4),
+            )
+
+        def quantize_dealt():
+            codes = keep.tile([P, KA, KP], U32, name="w1w_8", align_bytes=64)
+            scales = keep.tile([P, KA, KP], U8, name="w1s_8", align_bytes=64)
+            for a in range(KA):
+                quantize(codes[:, a, :], scales[:, a, :], dealt[a][:])
+                for t in range(4):
+                    cs = slice(P * t, P * (t + 1))
+                    w1_q[(a, SPLIT + t)] = (codes[:, a, cs], scales[:, a, cs])
+
+        waiting["w1w_8"] = quantize_dealt
+
+        def last_rows(src, s):
+            return src[P * SPLIT : H, :].rearrange("(p t) c -> p t c", t=4)[:, s - SPLIT, :]
+
         def prepare(loaded):
             for it, rows in loaded:
                 if it[0] == "w1":
                     prepare_w1(it[1], it[2], rows)
+                elif it[0] == "dealt":
+                    deal_w1(it[1], rows)
                 else:
                     b, c0, width = it[1:]
                     for c in range(0, width, 256):
                         round_rows(w4_g[:, b, 4 * (c0 + c) : 4 * (c0 + c + 256)], rows[:, :, c : c + 256])
 
         pages = {}
+        held = {}
 
         def put_slice(s):
             p1 = banks[s % 2]
             last = s == SLICES - 1
-            wg = ring.tile([P, S], F32, name="wg", tag="wg", bufs=SLICES - 1)
-            nc.scalar.activation(wg[:], wgs_sb[:], ACT.Copy, scale=gain_sb[:, s : s + 1])
+            if s == 2:
+                held["wg"] = ring.tile([P, 4, S], F32, name="wg_early", tag="early", bufs=1, align_bytes=64)
+            if s < 2:
+                wg = ring.tile([P, S], F32, name="wg", tag="bare")[:]
+            elif last:
+                wg = ring.tile([P, S], F32, name="wg", tag="late_w", bufs=1, align_bytes=64)[:]
+            else:
+                wg = held["wg"][:, (s - 2) % 4, :]
+            if s < SPLIT:
+                nc.scalar.activation(wg, wgs_sb[:], ACT.Copy, scale=gain_sb[:, s : s + 1])
+            else:
+                t = s - SPLIT
+                nc.scalar.activation(wg, wgs_last[:, t, :], ACT.Copy, scale=gain_last[:, t : t + 1])
             for a in range(KA):
                 codes, scales = w1_q[(a, s)]
                 nc.tensor.matmul_mx(
@@ -187,11 +232,11 @@ def tile_list_mattress_sag_page_kernel(
                     rhs=v_w[a][:].bitcast(FP8X4), rhs_scale=v_s[4 * a : P, :],
                     start=(a == 0), stop=(a == KA - 1),
                 )
-            h = ring.tile([P, S], F32, name="h", tag="late_h" if last else "h", bufs=1 if last else 2)
+            h = ring.tile([P, S], F32, name="h", tag=H_TAGS.get(s, "h"), bufs=1 if s in H_TAGS else 2, align_bytes=64)
             nc.scalar.activation(h[:], p1[:], ACT.Silu)
-            page = ring.tile([P, T2], F32, name="page", tag="page", bufs=5)
-            nc.sync.dma_start(page[:], page0[P * s : P * (s + 1), :])
-            nc.vector.tensor_tensor(page[:].indirect(idx2[:]), h[:], wg[:], MULT)
+            page = ring.tile([P, T2], F32, name="page", tag="page", bufs=6)
+            nc.sync.dma_start(page[:], page0[P * s : P * (s + 1), :] if s < SPLIT else last_rows(page0, s))
+            nc.vector.tensor_tensor(page[:].indirect(idx2[:]), h[:], wg, MULT)
             pages[s] = page
 
         x_t = {}
@@ -201,31 +246,40 @@ def tile_list_mattress_sag_page_kernel(
         def fetch(s, dst, j0, count):
             nc.vector.tensor_copy(dst, pages[s][:].indirect(idx3[:, j0 // 16 : (j0 + count) // 16]))
 
-        def turn(s, src, j0, count, bank):
+        def turn(s, bank):
             b, sl = divmod(s, 4)
-            if j0 == 0 and s in AFTER_TRIAL:
-                given = keep.tile([P, count], F32, name="given", tag=AFTER_TRIAL[s], align_bytes=64)
-            elif j0 == 0:
-                given = ring.tile([P, count], F32, name="given", tag="trial", bufs=3)
+            if s in AFTER_TRIAL:
+                given = keep.tile([P, S], F32, name="given", tag=AFTER_TRIAL[s], align_bytes=64)
             else:
-                given = ring.tile([P, count], F32, name="given", tag="trial_rest", bufs=4)
-            nc.sync.dma_start(given[:], trial[P * s : P * (s + 1), j0 : j0 + count])
-            for c in range(0, count, P):
-                nc.tensor.matmul(bank[:, c : c + P], given[:, c : c + P], ident[:],
-                                 start=(c == 0), stop=False, is_transpose=True)
-            for c in range(0, count, P):
-                nc.tensor.matmul(bank[:, c : c + P], src[:, c : c + P], ident[:],
-                                 start=False, stop=(c == count - P), is_transpose=True)
-            if b not in x_t:
-                x_t[b] = ring.tile([P, JT, 2, P, 2], BF16, name="xt", tag="xt", bufs=2)
+                given = ring.tile([P, S], F32, name="given", tag="trial", bufs=1)
+            nc.sync.dma_start(given[:], trial[P * s : P * (s + 1), :])
+            for i, src in enumerate((given, got)):
+                for c in range(0, S, P):
+                    nc.tensor.matmul(bank[:, c : c + P], src[:, c : c + P], ident[:],
+                                     start=(i == 0 and c == 0), stop=(i == 1 and c == S - P), is_transpose=True)
+            if sl == 0:
+                x_t[b] = ring.tile([P, JT, 2, P, 2], BF16, name="xt", tag="xt", bufs=1)
             nc.scalar.copy(
-                x_t[b][:, j0 // P : (j0 + count) // P, :, 32 * sl : 32 * (sl + 1), :],
-                bank[:, 0:count].rearrange("j (t p u e) -> j t u p e", p=32, u=2, e=2),
+                x_t[b][:, :, :, 32 * sl : 32 * (sl + 1), :],
+                bank[:].rearrange("j (t p u e) -> j t u p e", p=32, u=2, e=2),
+            )
+
+        given_last = {}
+
+        def load_trial_last(s):
+            given_last[s] = ring.tile([P, S], F32, name="given_last", tag="given_last", bufs=4)
+            nc.sync.dma_start(given_last[s][:], last_rows(trial, s))
+
+        def fetch_last(s, dst, half):
+            entries = idx3[:, HALF * half // 16 : HALF * (half + 1) // 16]
+            nc.vector.tensor_tensor(
+                dst[:, s - SPLIT, :], pages[s][:].indirect(entries),
+                given_last[s][:, HALF * half : HALF * (half + 1)], ADD,
             )
 
         def turn_back(b, half, xi):
             words = x_t[b][:].rearrange("j t u p e -> j (t u p e)").bitcast(F32)
-            back = psum.tile([P, 2, 2, P], F32, name="back", tag="tr")
+            back = psum.tile([P, 2, 2, P], F32, name="back", tag="tr", bufs=1)
             for t in range(2):
                 for u in range(2):
                     w0 = P * (2 * (2 * half + t) + u)
@@ -240,20 +294,33 @@ def tile_list_mattress_sag_page_kernel(
                 turn_back(b, half, xi[:, half, :])
 
             def finish():
-                x_w[b] = keep.tile([P, S], U32, name="x_%d" % b, align_bytes=64)
+                pool = keep if b == 0 else ring
+                x_w[b] = pool.tile([P, S], U32, name="x_%d" % b, bufs=1, align_bytes=64)
                 quantize(x_w[b][:], x_s[:, b, :], xi[:].rearrange("p h w -> p (h w)").bitcast(BF16))
 
             waiting["x_%d" % b] = finish
 
-        def finish_half(b, half):
-            xi = ring.tile([P, S], F32, name="xih", tag="later" if half == 0 else "xih", bufs=1, align_bytes=64)
-            turn_back(b, half, xi[:])
+        def finish_half(planes, half):
+            b = HA - 1
+            xi = ring.tile([P, 4 * HALF], BF16, name="xih", tag="later" if half == 0 else "xih", bufs=1, align_bytes=64)
+            round_rows(xi[:], planes[:])
             js = slice(HALF * half, HALF * (half + 1))
             if half == 0:
                 x_w[b] = keep.tile([P, S], U32, name="x_%d" % b, align_bytes=64)
-            quantize(x_w[b][:, js], x_s[:, b, js], xi[:].bitcast(BF16))
+            quantize(x_w[b][:, js], x_s[:, b, js], xi[:])
 
-        prepare(load_bulk((("w1", 0, 1),), "bounded", 2))
+        for a in range(KA):
+            raw = ring.tile([P, 4 * P], F32, name="raw", tag="bounded", align_bytes=64)
+            rows = load_rows(raw[:], w1, a, 0, P)
+            g = keep.tile([P, 4 * P], BF16, name="w1g_first%d" % a, align_bytes=64)
+            if a == 0:
+                round_rows(g[:], rows)
+            else:
+                nc.vector.tensor_copy(g[:].rearrange("p (c i) -> p c i", i=4), rows.rearrange("p i c -> p c i"))
+            codes = keep.tile([P, P], U32, name="w1w_first%d" % a, align_bytes=64)
+            scales = keep.tile([P, P], U8, name="w1s_first%d" % a, align_bytes=64)
+            quantize(codes[:], scales[:], g[:])
+            w1_q[(a, 0)] = (codes[:], scales[:])
         wgs_sb = keep.tile([P, S], F32, name="wgs_sb")
         nc.sync.dma_start(wgs_sb[:], wgs)
         idx2 = load_list(offs2, "idx2")
@@ -261,24 +328,30 @@ def tile_list_mattress_sag_page_kernel(
         w2_w = keep.tile([P, HA, 2 * N], U8, name="w2_w", align_bytes=64)
         w3_w = keep.tile([P, KA, N], U32, name="w3_w", align_bytes=64)
         ahead = {}
-        SPLIT = SLICES - 4
-        for s in range(SLICES + 2):
-            if s < SLICES:
-                put_slice(s)
+        first_half = keep.tile([P, 4, HALF], F32, name="first_half")
+        for s in range(SLICES):
+            put_slice(s)
             if s == 0:
-                prepare(load_bulk((("w1", 1, 2),)))
+                prepare(load_bulk((("w1", 1, 2),), "early", 1))
                 got = ring.tile([P, S], F32, name="got", tag="first", bufs=1, align_bytes=64)
-            if s >= 2:
-                width = S if s - 2 < SPLIT else HALF
-                g0 = HALF if s - 2 == SLICES - 2 else 0
-                turn(s - 2, got[:, g0 : g0 + width], 0, width, banks[s % 2])
-            if 1 <= s <= SLICES:
-                width = S if s - 1 < SPLIT else HALF
-                g0 = HALF if s - 1 == SLICES - 2 else 0
-                fetch(s - 1, got[:, g0 : g0 + width], 0, width)
+            if 2 <= s < SPLIT + 2:
+                turn(s - 2, banks[s % 2])
+            if 1 <= s <= SPLIT:
+                fetch(s - 1, got[:], 0, S)
+            for r in LAST_FETCH.get(s, ()):
+                load_trial_last(r)
+                fetch_last(r, first_half, 0)
+            if s == SLICES - 2:
+                waiting["x_1"]()
+            if s == 5:
+                wgs_last = ring.tile([P, 4, S], F32, name="wgs_last", tag="wgs_last", bufs=1)
+                for q in range(4):
+                    nc.sync.dma_start(wgs_last[32 * q : 32 * (q + 1), :, :], wgs.rearrange("(p t) j -> p t j", t=4))
+                gain_last = keep.tile([P, 4], F32, name="gain_last")
+                nc.sync.dma_start(gain_last[:], gain[P * SPLIT : H].rearrange("(p t) -> p t", t=4))
             if s - 2 in AFTER_TRIAL:
                 waiting[AFTER_TRIAL[s - 2]]()
-            for w in (() if s == 0 else (1, 2) if s == 1 else (3, 4) if s == 2 else (s + 2,)):
+            for w in LOADS.get(s, (s + 2,)):
                 if w in BULK:
                     ahead[w] = load_bulk(BULK[w])
             if s in BULK:
@@ -304,15 +377,15 @@ def tile_list_mattress_sag_page_kernel(
                 )
             if s in (5, 9):
                 finish_block((s - 5) // 4)
-        finish_half(HA - 1, 0)
-        rest = ring.tile([P, 4, HALF], F32, name="rest", tag="late_h", bufs=1)
+        finish_half(first_half, 0)
+        rest = ring.tile([P, 4, HALF], F32, name="rest", tag="late_h", bufs=1, align_bytes=64)
         for s in range(SPLIT, SLICES):
-            fetch(s, rest[:, s - SPLIT, :], HALF, HALF)
-            turn(s, rest[:, s - SPLIT, :], HALF, HALF, banks[s % 2])
-        w4_rest = ring.tile([P, HA, 512], U32, name="w4_rest", tag="later", bufs=1, align_bytes=64)
+            fetch_last(s, rest, 1)
+        w4_early = ring.tile([P, 512], U32, name="w4_early", tag="late_w", bufs=1, align_bytes=64)
+        w4_late = ring.tile([P, 2, 512], U32, name="w4_late", tag="later", bufs=1, align_bytes=64)
+        w4_rest = [w4_early[:], w4_late[:, 0, :], w4_late[:, 1, :]]
         for b in range(HA):
-            quantize(w4_rest[:, b, :], w4_s[:, b, 256:N], w4_g[:, b, 1024 : 4 * N])
-        w4_w.extend((w4_rest[:, :, 0:256], w4_rest[:, :, 256:512]))
+            quantize(w4_rest[b], w4_s[:, b, 256:N], w4_g[:, b, 1024 : 4 * N])
 
         idx4 = load_list(offs4, "idx4")
         wgo_sb = keep.tile([P, S], F32, name="wgo_sb")
@@ -322,47 +395,56 @@ def tile_list_mattress_sag_page_kernel(
             page = keep.tile([P, T2], F32, name="out_page%d" % n)
             nc.sync.dma_start(page[:], page1[P * n : P * (n + 1), :])
             out_pages.append(page)
-        for pair in range(NT // 2):
-            c0 = 2 * P * pair
-            cols = slice(c0, c0 + 2 * P)
-            for half in range(2):
-                if pair == 0 and half == 1:
-                    finish_half(HA - 1, 1)
-                p2 = psum.tile([P, 2, 2 * P], F32, name="p2", tag="y", bufs=4)
-                p4 = psum.tile([P, 2, 2 * P], F32, name="p4", tag="y", bufs=4)
-                tiles = [slice(HALF * half + P * t, HALF * half + P * (t + 1)) for t in range(2)]
-                for a in range(KA):
-                    for t, js in enumerate(tiles):
-                        nc.tensor.matmul_mx(
-                            p2[:, t, :], lhsT=v_w[a][:, js].bitcast(FP8X4), lhsT_scale=v_s[4 * a : P, js],
-                            rhs=w3_w[:, a, cols].bitcast(FP8X4), rhs_scale=w3_s[:, a, cols],
-                            start=(a == 0 and t == 0), stop=False,
-                        )
-                for b in range(HA):
-                    for t, js in enumerate(tiles):
-                        for i in range(2):
-                            n0 = c0 + P * i
-                            nc.tensor.matmul_mx(
-                                p2[:, t, P * i : P * (i + 1)],
-                                lhsT=x_w[b][:, js].bitcast(FP8X4), lhsT_scale=x_s[:, b, js],
-                                rhs=w2_w[:, b, 2 * n0 : 2 * (n0 + P)].bitcast(FP4X4),
-                                rhs_scale=w2_s[:, b, n0 : n0 + P],
-                                start=False, stop=(b == HA - 1 and t == 1 and i == 1),
-                            )
-                    for t, js in enumerate(tiles):
-                        nc.tensor.matmul_mx(
-                            p4[:, t, :], lhsT=x_w[b][:, js].bitcast(FP8X4), lhsT_scale=x_s[:, b, js],
-                            rhs=w4_w[pair][:, b, :].bitcast(FP8X4), rhs_scale=w4_s[:, b, cols],
-                            start=(b == 0 and t == 0), stop=(b == HA - 1 and t == 1),
-                        )
-                bounded = ring.tile([P, 2, 2 * P], F32, name="bounded", tag="bounded", align_bytes=64)
-                nc.scalar.activation(bounded[:], p2[:], ACT.Tanh)
+
+        def w4_codes(b, c0, width):
+            if c0 < 256:
+                return w4_w[0][:, b, c0 : c0 + width]
+            return w4_rest[b][:, c0 - 256 : c0 - 256 + width]
+
+        def operands(kind, a, n0, n_width, j0, j_width):
+            ns = slice(n0, n0 + n_width)
+            js = slice(j0, j0 + j_width)
+            if kind == "w3":
+                return (w3_w[:, a, ns].bitcast(FP8X4), w3_s[:, a, ns]), (v_w[a][:, js].bitcast(FP8X4), v_s[4 * a : P, js])
+            x = (x_w[a][:, js].bitcast(FP8X4), x_s[:, a, js])
+            if kind == "w2":
+                return (w2_w[:, a, 2 * n0 : 2 * (n0 + n_width)].bitcast(FP4X4), w2_s[:, a, ns]), x
+            return (w4_codes(a, n0, n_width).bitcast(FP8X4), w4_s[:, a, ns]), x
+
+        def products(bank, terms, pair, half, entries_on_partitions):
+            passes = []
+            for kind, a in terms:
+                width = P if kind == "w2" else 2 * P
+                for i in range(2):
+                    for c in range(0, 2 * P, width):
+                        if entries_on_partitions:
+                            w, x = operands(kind, a, 2 * P * pair + c, width, HALF * half + P * i, P)
+                            passes.append((bank[:, i, c : c + width], x, w))
+                        else:
+                            w, x = operands(kind, a, 2 * P * pair + P * i, P, HALF * half + c, width)
+                            passes.append((bank[:, i, c : c + width], w, x))
+            for i, (place, still, moving) in enumerate(passes):
+                nc.tensor.matmul_mx(place, lhsT=still[0], lhsT_scale=still[1], rhs=moving[0], rhs_scale=moving[1],
+                                    start=(i == 0), stop=(i == len(passes) - 1))
+
+        inside = [("w3", a) for a in range(KA)] + [("w2", b) for b in range(HA)]
+        beside = [("w4", b) for b in range(HA)]
+        for unit, (pair, half) in enumerate(UNITS):
+            if unit == 1:
+                finish_half(rest, 1)
+            p2 = psum.tile([P, 2, 2 * P], F32, name="p2", tag="p2", bufs=3)
+            p4 = psum.tile([P, 2, 2 * P], F32, name="p4", tag="p4", bufs=2)
+            products(p2, inside, pair, half, unit > 0)
+            products(p4, beside, pair, half, unit > 0)
+            bounded = ring.tile([P, 2, 2 * P], F32, name="bounded", tag="bounded", align_bytes=64)
+            nc.scalar.activation(bounded[:], p2[:], ACT.Tanh)
+            y = ring.tile([P, 2, HALF], F32, name="y", tag="y_sb")
+            if unit == 0:
+                nc.vector.tensor_tensor(y[:], p4[:], bounded[:], ADD)
+            else:
                 bare = ring.tile([P, 2, 2 * P], F32, name="bare", tag="bare")
-                if pair == 0 and half == 0:
-                    nc.vector.tensor_copy(bare[:], p4[:])
-                else:
-                    nc.scalar.copy(bare[:], p4[:])
-                y_ps = psum.tile([P, 2, 2, P], F32, name="y_ps", tag="tr")
+                nc.scalar.copy(bare[:], p4[:])
+                y_ps = banks[unit % 2][:].rearrange("p (i t j) -> p i t j", i=2, t=2)
                 for i in range(2):
                     for t in range(2):
                         ns = slice(P * i, P * (i + 1))
@@ -370,12 +452,11 @@ def tile_list_mattress_sag_page_kernel(
                                          start=True, stop=False, is_transpose=True)
                         nc.tensor.matmul(y_ps[:, i, t, :], bare[:, t, ns], ident[:],
                                          start=False, stop=True, is_transpose=True)
-                y = ring.tile([P, 2, HALF], F32, name="y", tag="y_sb")
-                nc.scalar.copy(y[:], y_ps[:].rearrange("p i t j -> p i (t j)"))
-                js = slice(HALF * half, HALF * (half + 1))
-                entries = idx4[:, HALF * half // 16 : HALF * (half + 1) // 16]
-                for i in range(2):
-                    n = 2 * pair + i
-                    nc.vector.tensor_tensor(out_pages[n][:].indirect(entries), y[:, i, :], wgo_sb[:, js], MULT)
-                    if half == 1:
-                        nc.sync.dma_start(out[P * n : P * (n + 1), :], out_pages[n][:])
+                nc.scalar.copy(y[:].rearrange("p i j -> p (i j)"), banks[unit % 2][:])
+            js = slice(HALF * half, HALF * (half + 1))
+            entries = idx4[:, HALF * half // 16 : HALF * (half + 1) // 16]
+            for i in range(2):
+                n = 2 * pair + i
+                nc.vector.tensor_tensor(out_pages[n][:].indirect(entries), y[:, i, :], wgo_sb[:, js], MULT)
+                if half == 1:
+                    nc.sync.dma_start(out[P * n : P * (n + 1), :], out_pages[n][:])

@@ -26,22 +26,15 @@ NT = N // P
 JT = S // P
 HALF = S // 2
 UNITS = ((0, 0), (1, 0), (0, 1), (1, 1), (2, 0), (2, 1))
-BULK = {
-    1: (("w1", 3, 2),),
-    2: (("w1", 5, 2),),
-    3: (("w1", 7, 1), ("w4", 0, 0, 256)),
-    4: (("dealt", 0),),
-    5: (("dealt", 1),),
-    6: (("w4", 1, 0, 256), ("w4", 2, 0, 256)),
-    7: (("w4", 0, 256, 512),),
-    8: (("w4", 1, 256, 512),),
-    10: (("w4", 2, 256, 512),),
-}
-AFTER_TRIAL = {1: "w1w_5", 3: "w1w_7", 4: "w1w_8", 5: "x_0", 6: "w4_first"}
 SPLIT = SLICES - 4
+LOADS = {1: ("pair0", "pair1"), 2: ("mid0", "mid1"), 3: ("dealt0",), 4: ("dealt1",), 5: ("first",), 6: ("w3",), 7: ("w2",), 8: ("scales", "rest0"), 10: ("rest1",), 11: ("rest2",)}
+ROUNDS = {1: (("w1", 3, 2),), 2: (("w1", 5, 2),), 3: (("w1", 7, 1),), 4: (("dealt", 0),), 5: (("dealt", 1),),
+          7: (("first",),), 9: (("rest", 0),), 11: (("rest", 1),), 12: (("rest", 2),)}
+DEAL_AT = 5
+AFTER_TRIAL = {1: "w1w_5", 2: "w1w_7", 4: "w1w_8", 5: "x_0", 6: "w4_first"}
 LAST_FETCH = {9: (8,), 10: (9, 10), 11: (11,)}
-LOADS = {0: (), 1: (1, 2), 2: (3,), 3: (4, 5)}
 H_TAGS = {SLICES - 2: "x_1", SLICES - 1: "late_h"}
+AL = 256
 
 
 def tile_list_mattress_sag_page_kernel(
@@ -70,7 +63,7 @@ def tile_list_mattress_sag_page_kernel(
         v_w = []
         v_s = keep.tile([P, S], U8, name="v_s", align_bytes=64)
         for a in range(KA):
-            tw = ring.tile([P, T], U32, name="tw", tag="raw", bufs=4, align_bytes=64)
+            tw = ring.tile([P, T], U32, name="tw", tag="raw", bufs=4, align_bytes=AL)
             nc.sync.dma_start(
                 tw[:].bitcast(I32), tab_words[a].rearrange("p t i -> p (t i)").bitcast(I32)
             )
@@ -129,24 +122,42 @@ def tile_list_mattress_sag_page_kernel(
             )
             return rows
 
-        def load_bulk(items, tag="raw", bufs=4):
-            size = sum(8 * P * it[2] if it[0] == "w1" else 4 * KP if it[0] == "dealt" else 4 * it[3] for it in items)
-            raw = ring.tile([P, size], F32, name="raw", tag=tag, bufs=bufs, align_bytes=64)
-            loaded = []
-            at = 0
-            for it in items:
-                if it[0] == "w1":
-                    width = P * it[2]
-                    rows = [load_rows(raw[:, at + 4 * width * a : at + 4 * width * (a + 1)], w1, a, P * it[1], width)
-                            for a in range(KA)]
-                    at = at + 8 * width
-                elif it[0] == "dealt":
-                    rows = load_rows(raw[:], w1, it[1], P * SPLIT, KP)
-                else:
-                    rows = load_rows(raw[:, at : at + 4 * it[3]], w4, it[1], it[2], it[3])
-                    at = at + 4 * it[3]
-                loaded.append((it, rows))
-            return loaded
+        raws = {}
+
+        def raw_tile(width):
+            return ring.tile([P, 4 * width], F32, name="raw", tag="raw", bufs=4, align_bytes=AL)
+
+        def load(what):
+            kind, a = what[:-1], what[-1]
+            if kind == "pair":
+                if a == "0":
+                    raws["pair"] = raw_tile(KP)
+                raws[what] = load_rows(raws["pair"][:, 1024 * int(a) : 1024 * (int(a) + 1)], w1, int(a), 3 * P, 2 * P)
+            elif kind == "mid":
+                raws[what] = load_rows(raw_tile(3 * P)[:], w1, int(a), 5 * P, 3 * P)
+            elif kind == "dealt":
+                raws[what] = load_rows(raw_tile(KP)[:], w1, int(a), P * SPLIT, KP)
+            elif kind == "rest":
+                raws[what] = load_rows(raw_tile(KP)[:], w4, int(a), 256, KP)
+            elif what == "first":
+                two = raw_tile(KP)
+                one = raw_tile(256)
+                raws[what] = [load_rows(dst, w4, b, 0, 256)
+                              for b, dst in enumerate((two[:, 0:1024], two[:, 1024:2048], one[:]))]
+            elif what == "w2":
+                nc.sync.dma_start(w2_w[:].bitcast(I32), w2_words.rearrange("a p c -> p a c").bitcast(I32))
+            elif what == "w3":
+                nc.sync.dma_start(w3_w[:].bitcast(I32), w3_words.rearrange("a p c i -> p a (c i)").bitcast(I32))
+            else:
+                for q in range(4):
+                    nc.sync.dma_start(
+                        w2_s[32 * q : 32 * q + 4, :, :].bitcast(I32),
+                        w2_scales[:, 4 * q : 4 * q + 4, :].rearrange("a r c -> r a c").bitcast(I32),
+                    )
+                    nc.sync.dma_start(
+                        w3_s[32 * q : 32 * q + 4, :, :].bitcast(I32),
+                        w3_scales[:, 4 * q : 4 * q + 4, :].rearrange("a r c -> r a c").bitcast(I32),
+                    )
 
         def prepare_w1(s0, count, rows):
             width = P * count
@@ -177,8 +188,8 @@ def tile_list_mattress_sag_page_kernel(
         def deal_w1(a, rows):
             dealt[a] = ring.tile([P, 4 * KP], BF16, name="w1g", tag="w1g", bufs=2, align_bytes=64)
             nc.scalar.copy(
-                dealt[a][:].rearrange("p (t m i) -> p m i t", t=4, i=4),
-                rows.rearrange("p i (m t) -> p m i t", t=4),
+                dealt[a][:].rearrange("p (t m i) -> p m t i", t=4, i=4),
+                rows.rearrange("p i (m t) -> p m t i", t=4),
             )
 
         def quantize_dealt():
@@ -195,16 +206,38 @@ def tile_list_mattress_sag_page_kernel(
         def last_rows(src, s):
             return src[P * SPLIT : H, :].rearrange("(p t) c -> p t c", t=4)[:, s - SPLIT, :]
 
-        def prepare(loaded):
-            for it, rows in loaded:
-                if it[0] == "w1":
-                    prepare_w1(it[1], it[2], rows)
-                elif it[0] == "dealt":
-                    deal_w1(it[1], rows)
-                else:
-                    b, c0, width = it[1:]
-                    for c in range(0, width, 256):
-                        round_rows(w4_g[:, b, 4 * (c0 + c) : 4 * (c0 + c + 256)], rows[:, :, c : c + 256])
+        def prepare(it):
+            if it[0] == "w1":
+                kind, c0 = ("pair", 0) if it[1] == 3 else ("mid", P * (it[1] - 5))
+                prepare_w1(it[1], it[2], [raws["%s%d" % (kind, a)][:, :, c0 : c0 + P * it[2]] for a in range(KA)])
+            elif it[0] == "dealt":
+                deal_w1(it[1], raws["dealt%d" % it[1]])
+            elif it[0] == "first":
+                for b in range(HA):
+                    round_rows(w4_g[:, b, 0:1024], raws["first"][b])
+            else:
+                for c in range(0, KP, 256):
+                    round_rows(w4_g[:, it[1], 1024 + 4 * c : 1024 + 4 * (c + 256)], raws["rest%d" % it[1]][:, :, c : c + 256])
+
+        def deal_wgs():
+            turned = psum.tile([P, JT, P], F32, name="turned", tag="tr", bufs=1)
+            for jt in range(JT):
+                nc.tensor.transpose(turned[:, jt, :], wgs_sb[:, P * jt : P * (jt + 1)], ident[:])
+            held["last"] = keep.tile([P, 3, S], F32, name="wg_last")
+            held["late"] = ring.tile([P, S], F32, name="wg", tag="late_w", bufs=1, align_bytes=64)
+            for t in range(4):
+                picked = keep.tile([P, JT, 4, 32], F32, name="picked")
+                nc.scalar.copy(
+                    picked[:],
+                    turned[:].rearrange("j a (p t) -> j t a p", t=4)[:, t, :, :].unsqueeze(2).to_broadcast([P, JT, 4, 32]),
+                )
+                rows = psum.tile([P, JT, P], F32, name="rows", tag="p2", bufs=3)
+                for jt in range(JT):
+                    nc.tensor.transpose(rows[:, jt, :], picked[:, jt, :, :].rearrange("j r p -> j (r p)"), ident[:])
+                nc.scalar.activation(
+                    held["last"][:, t, :] if t < 3 else held["late"][:], rows[:].rearrange("p a j -> p (a j)"),
+                    ACT.Copy, scale=gain_last[:, t : t + 1],
+                )
 
         pages = {}
         held = {}
@@ -213,18 +246,15 @@ def tile_list_mattress_sag_page_kernel(
             p1 = banks[s % 2]
             last = s == SLICES - 1
             if s == 2:
-                held["wg"] = ring.tile([P, 4, S], F32, name="wg_early", tag="early", bufs=1, align_bytes=64)
+                held["wg"] = ring.tile([P, SPLIT - 2, S], F32, name="wg_early", tag="early", bufs=1, align_bytes=AL)
             if s < 2:
                 wg = ring.tile([P, S], F32, name="wg", tag="bare")[:]
-            elif last:
-                wg = ring.tile([P, S], F32, name="wg", tag="late_w", bufs=1, align_bytes=64)[:]
+            elif s < SPLIT:
+                wg = held["wg"][:, s - 2, :]
             else:
-                wg = held["wg"][:, (s - 2) % 4, :]
+                wg = held["late"][:] if last else held["last"][:, s - SPLIT, :]
             if s < SPLIT:
                 nc.scalar.activation(wg, wgs_sb[:], ACT.Copy, scale=gain_sb[:, s : s + 1])
-            else:
-                t = s - SPLIT
-                nc.scalar.activation(wg, wgs_last[:, t, :], ACT.Copy, scale=gain_last[:, t : t + 1])
             for a in range(KA):
                 codes, scales = w1_q[(a, s)]
                 nc.tensor.matmul_mx(
@@ -234,7 +264,7 @@ def tile_list_mattress_sag_page_kernel(
                 )
             h = ring.tile([P, S], F32, name="h", tag=H_TAGS.get(s, "h"), bufs=1 if s in H_TAGS else 2, align_bytes=64)
             nc.scalar.activation(h[:], p1[:], ACT.Silu)
-            page = ring.tile([P, T2], F32, name="page", tag="page", bufs=6)
+            page = ring.tile([P, T2], F32, name="page", tag="page", bufs=5, align_bytes=AL)
             nc.sync.dma_start(page[:], page0[P * s : P * (s + 1), :] if s < SPLIT else last_rows(page0, s))
             nc.vector.tensor_tensor(page[:].indirect(idx2[:]), h[:], wg, MULT)
             pages[s] = page
@@ -327,12 +357,12 @@ def tile_list_mattress_sag_page_kernel(
         idx3 = load_list(offs3, "idx3")
         w2_w = keep.tile([P, HA, 2 * N], U8, name="w2_w", align_bytes=64)
         w3_w = keep.tile([P, KA, N], U32, name="w3_w", align_bytes=64)
-        ahead = {}
         first_half = keep.tile([P, 4, HALF], F32, name="first_half")
         for s in range(SLICES):
             put_slice(s)
             if s == 0:
-                prepare(load_bulk((("w1", 1, 2),), "early", 1))
+                early = ring.tile([P, KA, 8 * P], F32, name="early", tag="early", bufs=1, align_bytes=AL)
+                prepare_w1(1, 2, [load_rows(early[:, a, :], w1, a, P, 2 * P) for a in range(KA)])
                 got = ring.tile([P, S], F32, name="got", tag="first", bufs=1, align_bytes=64)
             if 2 <= s < SPLIT + 2:
                 turn(s - 2, banks[s % 2])
@@ -343,41 +373,22 @@ def tile_list_mattress_sag_page_kernel(
                 fetch_last(r, first_half, 0)
             if s == SLICES - 2:
                 waiting["x_1"]()
-            if s == 5:
-                wgs_last = ring.tile([P, 4, S], F32, name="wgs_last", tag="wgs_last", bufs=1)
-                for q in range(4):
-                    nc.sync.dma_start(wgs_last[32 * q : 32 * (q + 1), :, :], wgs.rearrange("(p t) j -> p t j", t=4))
+            if s == DEAL_AT:
                 gain_last = keep.tile([P, 4], F32, name="gain_last")
                 nc.sync.dma_start(gain_last[:], gain[P * SPLIT : H].rearrange("(p t) -> p t", t=4))
+            for what in LOADS.get(s, ()):
+                load(what)
+            for it in ROUNDS.get(s, ()):
+                prepare(it)
             if s - 2 in AFTER_TRIAL:
                 waiting[AFTER_TRIAL[s - 2]]()
-            for w in LOADS.get(s, (s + 2,)):
-                if w in BULK:
-                    ahead[w] = load_bulk(BULK[w])
-            if s in BULK:
-                prepare(ahead[s])
-            if s == 9:
-                for q in range(4):
-                    nc.sync.dma_start(
-                        w2_s[32 * q : 32 * q + 4, :, :].bitcast(I32),
-                        w2_scales[:, 4 * q : 4 * q + 4, :].rearrange("a r c -> r a c").bitcast(I32),
-                    )
-                    nc.sync.dma_start(
-                        w3_s[32 * q : 32 * q + 4, :, :].bitcast(I32),
-                        w3_scales[:, 4 * q : 4 * q + 4, :].rearrange("a r c -> r a c").bitcast(I32),
-                    )
-            if s == 8:
-                nc.sync.dma_start(
-                    w2_w[:].bitcast(I32), w2_words.rearrange("a p c -> p a c").bitcast(I32)
-                )
-            if s == 7:
-                nc.sync.dma_start(
-                    w3_w[:].bitcast(I32),
-                    w3_words.rearrange("a p c i -> p a (c i)").bitcast(I32),
-                )
             if s in (5, 9):
                 finish_block((s - 5) // 4)
+            if s == DEAL_AT:
+                deal_wgs()
         finish_half(first_half, 0)
+        for it in ROUNDS.get(SLICES, ()):
+            prepare(it)
         rest = ring.tile([P, 4, HALF], F32, name="rest", tag="late_h", bufs=1, align_bytes=64)
         for s in range(SPLIT, SLICES):
             fetch_last(s, rest, 1)
@@ -392,7 +403,7 @@ def tile_list_mattress_sag_page_kernel(
         nc.sync.dma_start(wgo_sb[:], wgo)
         out_pages = []
         for n in range(NT):
-            page = keep.tile([P, T2], F32, name="out_page%d" % n)
+            page = keep.tile([P, T2], F32, name="out_page%d" % n, align_bytes=AL)
             nc.sync.dma_start(page[:], page1[P * n : P * (n + 1), :])
             out_pages.append(page)
 

@@ -19,22 +19,31 @@ MULT = mybir.AluOpType.mult
 ADD = mybir.AluOpType.add
 
 P = 128
-KP = 512
-KA, HA = K // KP, H // KP
+PACK = 4
+PASS = P * PACK
+K_PASSES, R_PASSES = K // PASS, H // PASS
 SLICES = H // P
-NT = N // P
-JT = S // P
+DEALT = SLICES - PACK
+LAST = SLICES - 1
+J_TILES = S // P
 HALF = S // 2
+PAIR = 2 * P
+MX_ALIGN = 64
+DMA_ALIGN = 256
+
 UNITS = ((0, 0), (1, 0), (0, 1), (1, 1), (2, 0), (2, 1))
-SPLIT = SLICES - 4
-LOADS = {1: ("pair0", "pair1"), 2: ("mid0", "mid1"), 3: ("dealt0",), 4: ("dealt1",), 5: ("first",), 6: ("w3",), 7: ("w2",), 8: ("scales", "rest0"), 10: ("rest1",), 11: ("rest2",)}
-ROUNDS = {1: (("w1", 3, 2),), 2: (("w1", 5, 2),), 3: (("w1", 7, 1),), 4: (("dealt", 0),), 5: (("dealt", 1),),
-          7: (("first",),), 9: (("rest", 0),), 11: (("rest", 1),), 12: (("rest", 2),)}
-DEAL_AT = 5
-AFTER_TRIAL = {1: "w1w_5", 2: "w1w_7", 4: "w1w_8", 5: "x_0", 6: "w4_first"}
-LAST_FETCH = {9: (8,), 10: (9, 10), 11: (11,)}
-H_TAGS = {SLICES - 2: "x_1", SLICES - 1: "late_h"}
-AL = 256
+
+QUEUED_BEHIND = {
+    1: (("w1", 3, 2),), 2: (("w1", 5, 3),), 3: (("dealt", 0),), 4: (("dealt", 1),), 5: (("w4_first",),),
+    6: (("w3",),), 7: (("w2",),), 8: (("scales",), ("w4_rest", 0)), 9: (("w4_rest", 1),), 10: (("w4_rest", 2),),
+}
+ROUNDED_BESIDE = {
+    1: ("w1", 3, 2), 2: ("w1", 5, 2), 3: ("w1", 7, 1), 4: ("dealt", 0), 5: ("dealt", 1), 7: ("w4_first",),
+    9: ("w4_rest", 0), 10: ("w4_rest", 1), 11: ("w4_rest", 2),
+}
+CODES_AFTER_TRIAL = {1: "w1_5", 2: "w1_7", 4: "w1_dealt", 5: "x_0", 7: "w4_first"}
+FETCHED_BEHIND = {9: (8,), 10: (9, 10), 11: (11,)}
+H_TAGS = {LAST - 1: "x_1", LAST: "second_half"}
 
 
 def tile_list_mattress_sag_page_kernel(
@@ -49,368 +58,359 @@ def tile_list_mattress_sag_page_kernel(
         psum = ctx.enter_context(tc.psum_pool(name="psum", bufs=2))
 
         def load_list(src, name):
-            t = lists.tile([P, S // 16], U16, name=name)
-            nc.sync.dma_start(t[:], src)
-            return t
+            entries = lists.tile([P, S // 16], U16, name=name)
+            nc.sync.dma_start(entries[:], src)
+            return entries
+
+        def raw_tile(columns, dtype=F32):
+            return ring.tile([P, columns], dtype, name="raw", tag="raw", bufs=4, align_bytes=DMA_ALIGN)
+
+        def load_rows(dst, src, a, c0, width):
+            rows = dst.rearrange("p (i c) -> p i c", i=PACK)
+            block = src[PASS * a : PASS * (a + 1), c0 : c0 + width]
+            nc.sync.dma_start(rows, block.rearrange("(p i) c -> p i c", i=PACK))
+            return rows
+
+        def round_rows(dst, rows):
+            nc.scalar.copy(
+                dst.rearrange("p (c e i) -> p c i e", e=4, i=PACK),
+                rows.rearrange("p i (c e) -> p c i e", e=4),
+            )
+
+        def quantize(codes, scales, rounded):
+            nc.vector.quantize_mx(codes.bitcast(FP8X4), scales, rounded)
+
+        def dealt_rows(src, s):
+            return src[P * DEALT : H, :].rearrange("(p i) c -> p i c", i=PACK)[:, s - DEALT, :]
 
         idx = load_list(offs, "idx")
-        tab_s = keep.tile([P, T], U8, name="tab_s", align_bytes=64)
+        tab_s = keep.tile([P, T], U8, name="tab_s", align_bytes=MX_ALIGN)
         nc.gpsimd.memset(tab_s[:].bitcast(I32), 0)
         gain_rows = keep.tile([P, P], F32, name="gain_rows")
         nc.vector.memset(gain_rows[:], 0.0)
-        warm = keep.tile([P, 1], F32, name="warm")
-        nc.scalar.activation(warm[:], gain_rows[:, P - 1 : P], ACT.Silu)
+        zeros = keep.tile([P, 1], F32, name="zeros")
+        nc.vector.memset(zeros[:], 0.0)
+        no_bias = keep.tile([P, 1], F32, name="no_bias")
+        nc.scalar.activation(no_bias[:], zeros[:], ACT.Silu)
         v_w = []
-        v_s = keep.tile([P, S], U8, name="v_s", align_bytes=64)
-        for a in range(KA):
-            tw = ring.tile([P, T], U32, name="tw", tag="raw", bufs=4, align_bytes=AL)
-            nc.sync.dma_start(
-                tw[:].bitcast(I32), tab_words[a].rearrange("p t i -> p (t i)").bitcast(I32)
-            )
-            vw = keep.tile([P, S], U32, name="v_w%d" % a, align_bytes=64)
-            nc.vector.tensor_copy(vw[:], tw[:].indirect(idx[:]))
-            v_w.append(vw)
+        v_s = keep.tile([P, S], U8, name="v_s", align_bytes=MX_ALIGN)
+        for a in range(K_PASSES):
+            tab_w = raw_tile(T, U32)
+            nc.sync.dma_start(tab_w[:].bitcast(I32), tab_words[a].rearrange("p t i -> p (t i)").bitcast(I32))
+            picked_w = keep.tile([P, S], U32, name="v_w%d" % a, align_bytes=MX_ALIGN)
+            nc.vector.tensor_copy(picked_w[:], tab_w[:].indirect(idx[:]))
+            v_w.append(picked_w)
             if a == 0:
                 for q in range(4):
                     nc.sync.dma_start(
-                        tab_s[32 * q : 32 * q + 8, :].bitcast(I32),
+                        tab_s[32 * q : 32 * q + 4 * K_PASSES, :].bitcast(I32),
                         tab_scales[:, 4 * q : 4 * q + 4, :].bitcast(I32),
                     )
-                nc.sync.dma_start(gain_rows[0:SPLIT, :], gain[0 : P * SPLIT].rearrange("(s q) -> s q", q=P))
+                nc.sync.dma_start(gain_rows[0:DEALT, :], gain[0 : P * DEALT].rearrange("(s q) -> s q", q=P))
                 nc.vector.tensor_copy(v_s[:], tab_s[:].indirect(idx[:]))
 
         ident = keep.tile([P, P], F32, name="ident")
         make_identity(nc, ident[:])
-        w2_s = keep.tile([P, HA, N], U8, name="w2_s", align_bytes=64)
-        w3_s = keep.tile([P, KA, N], U8, name="w3_s", align_bytes=64)
+        w2_s = keep.tile([P, R_PASSES, N], U8, name="w2_s", align_bytes=MX_ALIGN)
+        w3_s = keep.tile([P, K_PASSES, N], U8, name="w3_s", align_bytes=MX_ALIGN)
         nc.gpsimd.memset(w2_s[:].rearrange("p a c -> p (a c)").bitcast(I32), 0)
         nc.gpsimd.memset(w3_s[:].rearrange("p a c -> p (a c)").bitcast(I32), 0)
 
         banks = [psum.tile([P, S], F32, name="bank%d" % i, bufs=1) for i in range(2)]
-        gain_ps = psum.tile([P, P], F32, name="gain_ps", tag="tr", bufs=1)
-        nc.tensor.transpose(gain_ps[:], gain_rows[:], ident[:])
-        gain_sb = keep.tile([P, SPLIT], F32, name="gain_sb")
-        nc.scalar.copy(gain_sb[:], gain_ps[:, 0:SPLIT])
-
-        def round_rows(dst, rows):
-            nc.scalar.copy(
-                dst.rearrange("p (c e i) -> p c i e", e=4, i=4),
-                rows.rearrange("p i (c e) -> p c i e", e=4),
-            )
-
-        def quantize(codes, scales, g):
-            nc.vector.quantize_mx(codes.bitcast(FP8X4), scales, g)
+        gain_turned = psum.tile([P, P], F32, name="gain_turned", tag="turn", bufs=1)
+        nc.tensor.transpose(gain_turned[:], gain_rows[:], ident[:])
+        gain_plain = keep.tile([P, DEALT], F32, name="gain_plain")
+        nc.scalar.copy(gain_plain[:], gain_turned[:, 0:DEALT])
 
         w1_q = {}
-        w4_g = keep.tile([P, HA, 4 * N], BF16, name="w4g", align_bytes=64)
-        w4_s = keep.tile([P, HA, N], U8, name="w4s", align_bytes=64)
+        w1_raw = {}
+        other_raw = {}
+        w1_dealt = {}
+        w4_rounded = keep.tile([P, R_PASSES, PACK * N], BF16, name="w4_rounded", align_bytes=MX_ALIGN)
+        w4_s = keep.tile([P, R_PASSES, N], U8, name="w4_s", align_bytes=MX_ALIGN)
+        w4_first = []
         waiting = {}
-        w4_w = []
 
-        def quantize_w4_first():
-            codes = keep.tile([P, HA, 256], U32, name="w4_first", align_bytes=64)
-            for b in range(HA):
-                quantize(codes[:, b, :], w4_s[:, b, 0:256], w4_g[:, b, 0:1024])
-            w4_w.append(codes[:])
-
-        waiting["w4_first"] = quantize_w4_first
-
-        def load_rows(dst, src, a, c0, width):
-            rows = dst.rearrange("p (i c) -> p i c", i=4)
-            nc.sync.dma_start(
-                rows, src[KP * a : KP * (a + 1), c0 : c0 + width].rearrange("(p i) c -> p i c", i=4)
-            )
-            return rows
-
-        raws = {}
-
-        def raw_tile(width):
-            return ring.tile([P, 4 * width], F32, name="raw", tag="raw", bufs=4, align_bytes=AL)
-
-        def load(what):
-            kind, a = what[:-1], what[-1]
-            if kind == "pair":
-                if a == "0":
-                    raws["pair"] = raw_tile(KP)
-                raws[what] = load_rows(raws["pair"][:, 1024 * int(a) : 1024 * (int(a) + 1)], w1, int(a), 3 * P, 2 * P)
-            elif kind == "mid":
-                raws[what] = load_rows(raw_tile(3 * P)[:], w1, int(a), 5 * P, 3 * P)
+        def load_group(kind, *args):
+            if kind == "w1":
+                s0, count = args
+                width = P * count
+                shared = raw_tile(K_PASSES * PACK * width) if K_PASSES * width <= PASS else None
+                for a in range(K_PASSES):
+                    if shared is None:
+                        dst = raw_tile(PACK * width)[:]
+                    else:
+                        dst = shared[:, PACK * width * a : PACK * width * (a + 1)]
+                    rows = load_rows(dst, w1, a, P * s0, width)
+                    for i in range(count):
+                        w1_raw[(a, s0 + i)] = (rows, P * i)
             elif kind == "dealt":
-                raws[what] = load_rows(raw_tile(KP)[:], w1, int(a), P * SPLIT, KP)
-            elif kind == "rest":
-                raws[what] = load_rows(raw_tile(KP)[:], w4, int(a), 256, KP)
-            elif what == "first":
-                two = raw_tile(KP)
-                one = raw_tile(256)
-                raws[what] = [load_rows(dst, w4, b, 0, 256)
-                              for b, dst in enumerate((two[:, 0:1024], two[:, 1024:2048], one[:]))]
-            elif what == "w2":
+                other_raw[(kind, args[0])] = load_rows(raw_tile(PACK * PASS)[:], w1, args[0], P * DEALT, PASS)
+            elif kind == "w4_first":
+                two = raw_tile(2 * PACK * PAIR)
+                one = raw_tile(PACK * PAIR)
+                for b, dst in enumerate((two[:, 0 : PACK * PAIR], two[:, PACK * PAIR : 2 * PACK * PAIR], one[:])):
+                    other_raw[(kind, b)] = load_rows(dst, w4, b, 0, PAIR)
+            elif kind == "w4_rest":
+                other_raw[(kind, args[0])] = load_rows(raw_tile(PACK * (N - PAIR))[:], w4, args[0], PAIR, N - PAIR)
+            elif kind == "w2":
                 nc.sync.dma_start(w2_w[:].bitcast(I32), w2_words.rearrange("a p c -> p a c").bitcast(I32))
-            elif what == "w3":
+            elif kind == "w3":
                 nc.sync.dma_start(w3_w[:].bitcast(I32), w3_words.rearrange("a p c i -> p a (c i)").bitcast(I32))
             else:
                 for q in range(4):
-                    nc.sync.dma_start(
-                        w2_s[32 * q : 32 * q + 4, :, :].bitcast(I32),
-                        w2_scales[:, 4 * q : 4 * q + 4, :].rearrange("a r c -> r a c").bitcast(I32),
-                    )
-                    nc.sync.dma_start(
-                        w3_s[32 * q : 32 * q + 4, :, :].bitcast(I32),
-                        w3_scales[:, 4 * q : 4 * q + 4, :].rearrange("a r c -> r a c").bitcast(I32),
-                    )
+                    for dst, src in ((w2_s, w2_scales), (w3_s, w3_scales)):
+                        nc.sync.dma_start(
+                            dst[32 * q : 32 * q + 4, :, :].bitcast(I32),
+                            src[:, 4 * q : 4 * q + 4, :].rearrange("a r c -> r a c").bitcast(I32),
+                        )
 
-        def prepare_w1(s0, count, rows):
+        def round_w1(s0, count, rows, tag, bufs):
             width = P * count
-            g = ring.tile([P, KA, 4 * width], BF16, name="w1g", tag="first" if s0 == 1 else "w1g",
-                          bufs=1 if s0 == 1 else 2, align_bytes=64)
-            for a in range(KA):
-                round_rows(g[:, a, :], rows[a])
+            rounded = ring.tile([P, K_PASSES, PACK * width], BF16, name="w1_rounded", tag=tag, bufs=bufs,
+                                align_bytes=MX_ALIGN)
+            for a in range(K_PASSES):
+                round_rows(rounded[:, a, :], rows[a])
 
             def finish():
-                codes = keep.tile([P, KA, width], U32, name="w1w_%d" % s0, align_bytes=64)
-                scales = keep.tile([P, KA, width], U8, name="w1s_%d" % s0, align_bytes=64)
-                quantize(
-                    codes[:].rearrange("p a c -> p (a c)"), scales[:].rearrange("p a c -> p (a c)"),
-                    g[:].rearrange("p a c -> p (a c)"),
-                )
-                for a in range(KA):
+                codes = keep.tile([P, K_PASSES, width], U32, name="w1_w", tag="w1_%d" % s0, align_bytes=MX_ALIGN)
+                scales = keep.tile([P, K_PASSES, width], U8, name="w1_s%d" % s0, align_bytes=MX_ALIGN)
+                quantize(*(t[:].rearrange("p a c -> p (a c)") for t in (codes, scales, rounded)))
+                for a in range(K_PASSES):
                     for i in range(count):
-                        cs = slice(P * i, P * (i + 1))
-                        w1_q[(a, s0 + i)] = (codes[:, a, cs], scales[:, a, cs])
+                        cols = slice(P * i, P * (i + 1))
+                        w1_q[(a, s0 + i)] = (codes[:, a, cols], scales[:, a, cols])
 
-            if s0 < 5:
-                finish()
-            else:
-                waiting["w1w_%d" % s0] = finish
+            return finish
 
-        dealt = {}
+        def quantize_w1_dealt():
+            codes = keep.tile([P, K_PASSES, PASS], U32, name="w1_w", tag="w1_dealt", align_bytes=MX_ALIGN)
+            scales = keep.tile([P, K_PASSES, PASS], U8, name="w1_s_dealt", align_bytes=MX_ALIGN)
+            for a in range(K_PASSES):
+                quantize(codes[:, a, :], scales[:, a, :], w1_dealt[a][:])
+                for i in range(PACK):
+                    cols = slice(P * i, P * (i + 1))
+                    w1_q[(a, DEALT + i)] = (codes[:, a, cols], scales[:, a, cols])
 
-        def deal_w1(a, rows):
-            dealt[a] = ring.tile([P, 4 * KP], BF16, name="w1g", tag="w1g", bufs=2, align_bytes=64)
-            nc.scalar.copy(
-                dealt[a][:].rearrange("p (t m i) -> p m t i", t=4, i=4),
-                rows.rearrange("p i (m t) -> p m t i", t=4),
-            )
+        def quantize_w4_first():
+            codes = keep.tile([P, R_PASSES, PAIR], U32, name="w4_w", tag="w4_first", align_bytes=MX_ALIGN)
+            for b in range(R_PASSES):
+                quantize(codes[:, b, :], w4_s[:, b, 0:PAIR], w4_rounded[:, b, 0 : PACK * PAIR])
+                w4_first.append(codes[:, b, :])
 
-        def quantize_dealt():
-            codes = keep.tile([P, KA, KP], U32, name="w1w_8", align_bytes=64)
-            scales = keep.tile([P, KA, KP], U8, name="w1s_8", align_bytes=64)
-            for a in range(KA):
-                quantize(codes[:, a, :], scales[:, a, :], dealt[a][:])
-                for t in range(4):
-                    cs = slice(P * t, P * (t + 1))
-                    w1_q[(a, SPLIT + t)] = (codes[:, a, cs], scales[:, a, cs])
+        waiting["w1_dealt"] = quantize_w1_dealt
+        waiting["w4_first"] = quantize_w4_first
 
-        waiting["w1w_8"] = quantize_dealt
-
-        def last_rows(src, s):
-            return src[P * SPLIT : H, :].rearrange("(p t) c -> p t c", t=4)[:, s - SPLIT, :]
-
-        def prepare(it):
-            if it[0] == "w1":
-                kind, c0 = ("pair", 0) if it[1] == 3 else ("mid", P * (it[1] - 5))
-                prepare_w1(it[1], it[2], [raws["%s%d" % (kind, a)][:, :, c0 : c0 + P * it[2]] for a in range(KA)])
-            elif it[0] == "dealt":
-                deal_w1(it[1], raws["dealt%d" % it[1]])
-            elif it[0] == "first":
-                for b in range(HA):
-                    round_rows(w4_g[:, b, 0:1024], raws["first"][b])
-            else:
-                for c in range(0, KP, 256):
-                    round_rows(w4_g[:, it[1], 1024 + 4 * c : 1024 + 4 * (c + 256)], raws["rest%d" % it[1]][:, :, c : c + 256])
-
-        def deal_wgs():
-            turned = psum.tile([P, JT, P], F32, name="turned", tag="tr", bufs=1)
-            for jt in range(JT):
-                nc.tensor.transpose(turned[:, jt, :], wgs_sb[:, P * jt : P * (jt + 1)], ident[:])
-            held["last"] = keep.tile([P, 3, S], F32, name="wg_last")
-            held["late"] = ring.tile([P, S], F32, name="wg", tag="late_w", bufs=1, align_bytes=64)
-            for t in range(4):
-                picked = keep.tile([P, JT, 4, 32], F32, name="picked")
+        def round_group(kind, *args):
+            if kind == "w1":
+                s0, count = args
+                rows = []
+                for a in range(K_PASSES):
+                    loaded, c0 = w1_raw[(a, s0)]
+                    rows.append(loaded[:, :, c0 : c0 + P * count])
+                finish = round_w1(s0, count, rows, "w1_rounded", 2)
+                if "w1_%d" % s0 in CODES_AFTER_TRIAL.values():
+                    waiting["w1_%d" % s0] = finish
+                else:
+                    finish()
+            elif kind == "dealt":
+                a = args[0]
+                w1_dealt[a] = ring.tile([P, PACK * PASS], BF16, name="w1_rounded", tag="w1_rounded", bufs=2,
+                                        align_bytes=MX_ALIGN)
                 nc.scalar.copy(
-                    picked[:],
-                    turned[:].rearrange("j a (p t) -> j t a p", t=4)[:, t, :, :].unsqueeze(2).to_broadcast([P, JT, 4, 32]),
+                    w1_dealt[a][:].rearrange("p (t m i) -> p m t i", t=PACK, i=PACK),
+                    other_raw[(kind, a)].rearrange("p i (m t) -> p m t i", t=PACK),
                 )
-                rows = psum.tile([P, JT, P], F32, name="rows", tag="p2", bufs=3)
-                for jt in range(JT):
-                    nc.tensor.transpose(rows[:, jt, :], picked[:, jt, :, :].rearrange("j r p -> j (r p)"), ident[:])
-                nc.scalar.activation(
-                    held["last"][:, t, :] if t < 3 else held["late"][:], rows[:].rearrange("p a j -> p (a j)"),
-                    ACT.Copy, scale=gain_last[:, t : t + 1],
-                )
+            elif kind == "w4_first":
+                for b in range(R_PASSES):
+                    round_rows(w4_rounded[:, b, 0 : PACK * PAIR], other_raw[(kind, b)])
+            else:
+                b = args[0]
+                for c in range(PAIR, N, PAIR):
+                    round_rows(
+                        w4_rounded[:, b, PACK * c : PACK * (c + PAIR)],
+                        other_raw[(kind, b)][:, :, c - PAIR : c],
+                    )
 
+        factors = {}
         pages = {}
-        held = {}
+
+        def deal_factors():
+            turned = psum.tile([P, J_TILES, P], F32, name="turned", tag="turn", bufs=1)
+            for jt in range(J_TILES):
+                nc.tensor.transpose(turned[:, jt, :], wgs_sb[:, P * jt : P * (jt + 1)], ident[:])
+            three = keep.tile([P, PACK - 1, S], F32, name="factors_dealt")
+            fourth = ring.tile([P, S], F32, name="factors_last", tag="w4_early", bufs=1, align_bytes=MX_ALIGN)
+            for i in range(PACK):
+                repeated = keep.tile([P, J_TILES, 4, 32], F32, name="repeated")
+                every_fourth = turned[:].rearrange("j a (p i) -> j i a p", i=PACK)[:, i, :, :]
+                nc.scalar.copy(repeated[:], every_fourth.unsqueeze(2).to_broadcast([P, J_TILES, 4, 32]))
+                rows = psum.tile([P, J_TILES, P], F32, name="rows", tag="inside", bufs=3)
+                for jt in range(J_TILES):
+                    nc.tensor.transpose(rows[:, jt, :], repeated[:, jt, :, :].rearrange("j r p -> j (r p)"), ident[:])
+                factors[DEALT + i] = three[:, i, :] if i < PACK - 1 else fourth[:]
+                nc.scalar.activation(
+                    factors[DEALT + i], rows[:].rearrange("p a j -> p (a j)"), ACT.Copy, scale=gain_dealt[:, i : i + 1]
+                )
 
         def put_slice(s):
-            p1 = banks[s % 2]
-            last = s == SLICES - 1
-            if s == 2:
-                held["wg"] = ring.tile([P, SPLIT - 2, S], F32, name="wg_early", tag="early", bufs=1, align_bytes=AL)
-            if s < 2:
-                wg = ring.tile([P, S], F32, name="wg", tag="bare")[:]
-            elif s < SPLIT:
-                wg = held["wg"][:, s - 2, :]
-            else:
-                wg = held["late"][:] if last else held["last"][:, s - SPLIT, :]
-            if s < SPLIT:
-                nc.scalar.activation(wg, wgs_sb[:], ACT.Copy, scale=gain_sb[:, s : s + 1])
-            for a in range(KA):
+            product = banks[s % 2]
+            if s < DEALT:
+                nc.scalar.activation(factors[s], wgs_sb[:], ACT.Copy, scale=gain_plain[:, s : s + 1])
+            for a in range(K_PASSES):
                 codes, scales = w1_q[(a, s)]
                 nc.tensor.matmul_mx(
-                    p1[:], lhsT=codes.bitcast(FP8X4), lhsT_scale=scales,
+                    product[:], lhsT=codes.bitcast(FP8X4), lhsT_scale=scales,
                     rhs=v_w[a][:].bitcast(FP8X4), rhs_scale=v_s[4 * a : P, :],
-                    start=(a == 0), stop=(a == KA - 1),
+                    start=(a == 0), stop=(a == K_PASSES - 1),
                 )
-            h = ring.tile([P, S], F32, name="h", tag=H_TAGS.get(s, "h"), bufs=1 if s in H_TAGS else 2, align_bytes=64)
-            nc.scalar.activation(h[:], p1[:], ACT.Silu)
-            page = ring.tile([P, T2], F32, name="page", tag="page", bufs=5, align_bytes=AL)
-            nc.sync.dma_start(page[:], page0[P * s : P * (s + 1), :] if s < SPLIT else last_rows(page0, s))
-            nc.vector.tensor_tensor(page[:].indirect(idx2[:]), h[:], wg, MULT)
+            h = ring.tile([P, S], F32, name="h", tag=H_TAGS.get(s, "h"), bufs=1 if s in H_TAGS else 2,
+                          align_bytes=MX_ALIGN)
+            nc.scalar.activation(h[:], product[:], ACT.Silu, bias=no_bias[:] if s == 0 else 0.0)
+            page = ring.tile([P, T2], F32, name="page", tag="page", bufs=5, align_bytes=DMA_ALIGN)
+            nc.sync.dma_start(page[:], page0[P * s : P * (s + 1), :] if s < DEALT else dealt_rows(page0, s))
+            nc.vector.tensor_tensor(page[:].indirect(idx2[:]), h[:], factors[s], MULT)
             pages[s] = page
 
-        x_t = {}
+        x_turned = {}
         x_w = {}
-        x_s = keep.tile([P, HA, S], U8, name="x_s", align_bytes=64)
-
-        def fetch(s, dst, j0, count):
-            nc.vector.tensor_copy(dst, pages[s][:].indirect(idx3[:, j0 // 16 : (j0 + count) // 16]))
+        x_s = keep.tile([P, R_PASSES, S], U8, name="x_s", align_bytes=MX_ALIGN)
 
         def turn(s, bank):
-            b, sl = divmod(s, 4)
-            if s in AFTER_TRIAL:
-                given = keep.tile([P, S], F32, name="given", tag=AFTER_TRIAL[s], align_bytes=64)
+            b, quarter = divmod(s, PACK)
+            if s in CODES_AFTER_TRIAL:
+                given = keep.tile([P, S], F32, name="given", tag=CODES_AFTER_TRIAL[s], align_bytes=MX_ALIGN)
             else:
-                given = ring.tile([P, S], F32, name="given", tag="trial", bufs=1)
+                given = ring.tile([P, S], F32, name="given", tag="given", bufs=1)
             nc.sync.dma_start(given[:], trial[P * s : P * (s + 1), :])
-            for i, src in enumerate((given, got)):
+            for i, src in enumerate((given, fetched)):
                 for c in range(0, S, P):
                     nc.tensor.matmul(bank[:, c : c + P], src[:, c : c + P], ident[:],
                                      start=(i == 0 and c == 0), stop=(i == 1 and c == S - P), is_transpose=True)
-            if sl == 0:
-                x_t[b] = ring.tile([P, JT, 2, P, 2], BF16, name="xt", tag="xt", bufs=1)
+            if quarter == 0:
+                x_turned[b] = ring.tile([P, J_TILES, 2, P, 2], BF16, name="x_turned", tag="x_turned", bufs=1)
             nc.scalar.copy(
-                x_t[b][:, :, :, 32 * sl : 32 * (sl + 1), :],
+                x_turned[b][:, :, :, 32 * quarter : 32 * (quarter + 1), :],
                 bank[:].rearrange("j (t p u e) -> j t u p e", p=32, u=2, e=2),
             )
 
-        given_last = {}
-
-        def load_trial_last(s):
-            given_last[s] = ring.tile([P, S], F32, name="given_last", tag="given_last", bufs=4)
-            nc.sync.dma_start(given_last[s][:], last_rows(trial, s))
-
-        def fetch_last(s, dst, half):
-            entries = idx3[:, HALF * half // 16 : HALF * (half + 1) // 16]
-            nc.vector.tensor_tensor(
-                dst[:, s - SPLIT, :], pages[s][:].indirect(entries),
-                given_last[s][:, HALF * half : HALF * (half + 1)], ADD,
-            )
-
-        def turn_back(b, half, xi):
-            words = x_t[b][:].rearrange("j t u p e -> j (t u p e)").bitcast(F32)
-            back = psum.tile([P, 2, 2, P], F32, name="back", tag="tr", bufs=1)
-            for t in range(2):
-                for u in range(2):
-                    w0 = P * (2 * (2 * half + t) + u)
-                    nc.tensor.transpose(back[:, t, u, :], words[:, w0 : w0 + P], ident[:])
-            nc.scalar.copy(
-                xi.rearrange("p (t j u) -> p t j u", t=2, u=2), back[:].rearrange("p t u j -> p t j u")
-            )
-
-        def finish_block(b):
-            xi = ring.tile([P, 2, S], F32, name="xi", tag="xi", bufs=1, align_bytes=64)
+        def turn_back(b):
+            words = x_turned[b][:].rearrange("j t u p e -> j (t u p e)").bitcast(F32)
+            rounded = ring.tile([P, 2, S], F32, name="x_rounded", tag="x_rounded", bufs=1, align_bytes=MX_ALIGN)
             for half in range(2):
-                turn_back(b, half, xi[:, half, :])
+                back = psum.tile([P, 2, 2, P], F32, name="back", tag="turn", bufs=1)
+                for t in range(2):
+                    for u in range(2):
+                        w0 = P * (2 * (2 * half + t) + u)
+                        nc.tensor.transpose(back[:, t, u, :], words[:, w0 : w0 + P], ident[:])
+                nc.scalar.copy(
+                    rounded[:, half, :].rearrange("p (t j u) -> p t j u", t=2, u=2),
+                    back[:].rearrange("p t u j -> p t j u"),
+                )
 
             def finish():
                 pool = keep if b == 0 else ring
-                x_w[b] = pool.tile([P, S], U32, name="x_%d" % b, bufs=1, align_bytes=64)
-                quantize(x_w[b][:], x_s[:, b, :], xi[:].rearrange("p h w -> p (h w)").bitcast(BF16))
+                x_w[b] = pool.tile([P, S], U32, name="x_w", tag="x_%d" % b, bufs=1, align_bytes=MX_ALIGN)
+                quantize(x_w[b][:], x_s[:, b, :], rounded[:].rearrange("p h w -> p (h w)").bitcast(BF16))
 
             waiting["x_%d" % b] = finish
 
-        def finish_half(planes, half):
-            b = HA - 1
-            xi = ring.tile([P, 4 * HALF], BF16, name="xih", tag="later" if half == 0 else "xih", bufs=1, align_bytes=64)
-            round_rows(xi[:], planes[:])
+        given_dealt = {}
+
+        def fetch_dealt(s, dst, half):
+            entries = idx3[:, HALF * half // 16 : HALF * (half + 1) // 16]
+            nc.vector.tensor_tensor(
+                dst[:, s - DEALT, :], pages[s][:].indirect(entries),
+                given_dealt[s][:, HALF * half : HALF * (half + 1)], ADD,
+            )
+
+        def finish_half(summed, half, tag):
+            b = R_PASSES - 1
+            rounded = ring.tile([P, PACK * HALF], BF16, name="x_half", tag=tag, bufs=1, align_bytes=MX_ALIGN)
+            round_rows(rounded[:], summed[:])
             js = slice(HALF * half, HALF * (half + 1))
             if half == 0:
-                x_w[b] = keep.tile([P, S], U32, name="x_%d" % b, align_bytes=64)
-            quantize(x_w[b][:, js], x_s[:, b, js], xi[:])
+                x_w[b] = keep.tile([P, S], U32, name="x_w", tag="x_%d" % b, align_bytes=MX_ALIGN)
+            quantize(x_w[b][:, js], x_s[:, b, js], rounded[:])
 
-        for a in range(KA):
-            raw = ring.tile([P, 4 * P], F32, name="raw", tag="bounded", align_bytes=64)
+        for a in range(K_PASSES):
+            raw = ring.tile([P, PACK * P], F32, name="raw_first", tag="bounded", align_bytes=MX_ALIGN)
             rows = load_rows(raw[:], w1, a, 0, P)
-            g = keep.tile([P, 4 * P], BF16, name="w1g_first%d" % a, align_bytes=64)
+            rounded = keep.tile([P, PACK * P], BF16, name="w1_first%d" % a, align_bytes=MX_ALIGN)
             if a == 0:
-                round_rows(g[:], rows)
+                round_rows(rounded[:], rows)
             else:
-                nc.vector.tensor_copy(g[:].rearrange("p (c i) -> p c i", i=4), rows.rearrange("p i c -> p c i"))
-            codes = keep.tile([P, P], U32, name="w1w_first%d" % a, align_bytes=64)
-            scales = keep.tile([P, P], U8, name="w1s_first%d" % a, align_bytes=64)
-            quantize(codes[:], scales[:], g[:])
+                nc.vector.tensor_copy(
+                    rounded[:].rearrange("p (c i) -> p c i", i=PACK), rows.rearrange("p i c -> p c i")
+                )
+            codes = keep.tile([P, P], U32, name="w1_w_first%d" % a, align_bytes=MX_ALIGN)
+            scales = keep.tile([P, P], U8, name="w1_s_first%d" % a, align_bytes=MX_ALIGN)
+            quantize(codes[:], scales[:], rounded[:])
             w1_q[(a, 0)] = (codes[:], scales[:])
         wgs_sb = keep.tile([P, S], F32, name="wgs_sb")
         nc.sync.dma_start(wgs_sb[:], wgs)
         idx2 = load_list(offs2, "idx2")
         idx3 = load_list(offs3, "idx3")
-        w2_w = keep.tile([P, HA, 2 * N], U8, name="w2_w", align_bytes=64)
-        w3_w = keep.tile([P, KA, N], U32, name="w3_w", align_bytes=64)
-        first_half = keep.tile([P, 4, HALF], F32, name="first_half")
+        w2_w = keep.tile([P, R_PASSES, 2 * N], U8, name="w2_w", align_bytes=MX_ALIGN)
+        w3_w = keep.tile([P, K_PASSES, N], U32, name="w3_w", align_bytes=MX_ALIGN)
+        first_half = keep.tile([P, PACK, HALF], F32, name="first_half")
         for s in range(SLICES):
+            if s < 2:
+                factors[s] = ring.tile([P, S], F32, name="factors", tag="bare")[:]
+            if s == 2:
+                later = ring.tile([P, DEALT - 2, S], F32, name="factors", tag="early", bufs=1, align_bytes=DMA_ALIGN)
+                for r in range(2, DEALT):
+                    factors[r] = later[:, r - 2, :]
             put_slice(s)
             if s == 0:
-                early = ring.tile([P, KA, 8 * P], F32, name="early", tag="early", bufs=1, align_bytes=AL)
-                prepare_w1(1, 2, [load_rows(early[:, a, :], w1, a, P, 2 * P) for a in range(KA)])
-                got = ring.tile([P, S], F32, name="got", tag="first", bufs=1, align_bytes=64)
-            if 2 <= s < SPLIT + 2:
+                early = ring.tile([P, K_PASSES, PACK * 2 * P], F32, name="early", tag="early", bufs=1,
+                                  align_bytes=DMA_ALIGN)
+                rows = [load_rows(early[:, a, :], w1, a, P, 2 * P) for a in range(K_PASSES)]
+                round_w1(1, 2, rows, "fetched", 1)()
+                fetched = ring.tile([P, S], F32, name="fetched", tag="fetched", bufs=1, align_bytes=MX_ALIGN)
+            if 2 <= s < DEALT + 2:
                 turn(s - 2, banks[s % 2])
-            if 1 <= s <= SPLIT:
-                fetch(s - 1, got[:], 0, S)
-            for r in LAST_FETCH.get(s, ()):
-                load_trial_last(r)
-                fetch_last(r, first_half, 0)
-            if s == SLICES - 2:
-                waiting["x_1"]()
-            if s == DEAL_AT:
-                gain_last = keep.tile([P, 4], F32, name="gain_last")
-                nc.sync.dma_start(gain_last[:], gain[P * SPLIT : H].rearrange("(p t) -> p t", t=4))
-            for what in LOADS.get(s, ()):
-                load(what)
-            for it in ROUNDS.get(s, ()):
-                prepare(it)
-            if s - 2 in AFTER_TRIAL:
-                waiting[AFTER_TRIAL[s - 2]]()
-            if s in (5, 9):
-                finish_block((s - 5) // 4)
-            if s == DEAL_AT:
-                deal_wgs()
-        finish_half(first_half, 0)
-        for it in ROUNDS.get(SLICES, ()):
-            prepare(it)
-        rest = ring.tile([P, 4, HALF], F32, name="rest", tag="late_h", bufs=1, align_bytes=64)
-        for s in range(SPLIT, SLICES):
-            fetch_last(s, rest, 1)
-        w4_early = ring.tile([P, 512], U32, name="w4_early", tag="late_w", bufs=1, align_bytes=64)
-        w4_late = ring.tile([P, 2, 512], U32, name="w4_late", tag="later", bufs=1, align_bytes=64)
+            if 1 <= s <= DEALT:
+                nc.vector.tensor_copy(fetched[:], pages[s - 1][:].indirect(idx3[:]))
+            for r in FETCHED_BEHIND.get(s, ()):
+                given_dealt[r] = ring.tile([P, S], F32, name="given_dealt", tag="given_dealt", bufs=PACK)
+                nc.sync.dma_start(given_dealt[r][:], dealt_rows(trial, r))
+                fetch_dealt(r, first_half, 0)
+            if H_TAGS.get(s) in waiting:
+                waiting[H_TAGS[s]]()
+            if s == PACK + 1:
+                gain_dealt = keep.tile([P, PACK], F32, name="gain_dealt")
+                nc.sync.dma_start(gain_dealt[:], gain[P * DEALT : H].rearrange("(p i) -> p i", i=PACK))
+            for group in QUEUED_BEHIND.get(s, ()):
+                load_group(*group)
+            if s in ROUNDED_BESIDE:
+                round_group(*ROUNDED_BESIDE[s])
+            if s - 2 in CODES_AFTER_TRIAL:
+                waiting[CODES_AFTER_TRIAL[s - 2]]()
+            if s > PACK and s % PACK == 1:
+                turn_back(s // PACK - 1)
+            if s == PACK + 1:
+                deal_factors()
+
+        finish_half(first_half, 0, "w4_late")
+        second_half = ring.tile([P, PACK, HALF], F32, name="second_half", tag="second_half", bufs=1,
+                                align_bytes=MX_ALIGN)
+        for s in range(DEALT, SLICES):
+            fetch_dealt(s, second_half, 1)
+        w4_early = ring.tile([P, N - PAIR], U32, name="w4_early", tag="w4_early", bufs=1, align_bytes=MX_ALIGN)
+        w4_late = ring.tile([P, 2, N - PAIR], U32, name="w4_late", tag="w4_late", bufs=1, align_bytes=MX_ALIGN)
         w4_rest = [w4_early[:], w4_late[:, 0, :], w4_late[:, 1, :]]
-        for b in range(HA):
-            quantize(w4_rest[b], w4_s[:, b, 256:N], w4_g[:, b, 1024 : 4 * N])
+        for b in range(R_PASSES):
+            quantize(w4_rest[b], w4_s[:, b, PAIR:N], w4_rounded[:, b, PACK * PAIR : PACK * N])
 
         idx4 = load_list(offs4, "idx4")
         wgo_sb = keep.tile([P, S], F32, name="wgo_sb")
         nc.sync.dma_start(wgo_sb[:], wgo)
         out_pages = []
-        for n in range(NT):
-            page = keep.tile([P, T2], F32, name="out_page%d" % n, align_bytes=AL)
-            nc.sync.dma_start(page[:], page1[P * n : P * (n + 1), :])
-            out_pages.append(page)
-
-        def w4_codes(b, c0, width):
-            if c0 < 256:
-                return w4_w[0][:, b, c0 : c0 + width]
-            return w4_rest[b][:, c0 - 256 : c0 - 256 + width]
+        for n in range(N // P):
+            out_page = keep.tile([P, T2], F32, name="out_page%d" % n, align_bytes=DMA_ALIGN)
+            nc.sync.dma_start(out_page[:], page1[P * n : P * (n + 1), :])
+            out_pages.append(out_page)
 
         def operands(kind, a, n0, n_width, j0, j_width):
             ns = slice(n0, n0 + n_width)
@@ -420,48 +420,48 @@ def tile_list_mattress_sag_page_kernel(
             x = (x_w[a][:, js].bitcast(FP8X4), x_s[:, a, js])
             if kind == "w2":
                 return (w2_w[:, a, 2 * n0 : 2 * (n0 + n_width)].bitcast(FP4X4), w2_s[:, a, ns]), x
-            return (w4_codes(a, n0, n_width).bitcast(FP8X4), w4_s[:, a, ns]), x
+            codes = w4_first[a][:, ns] if n0 < PAIR else w4_rest[a][:, n0 - PAIR : n0 - PAIR + n_width]
+            return (codes.bitcast(FP8X4), w4_s[:, a, ns]), x
 
         def products(bank, terms, pair, half, entries_on_partitions):
             passes = []
             for kind, a in terms:
-                width = P if kind == "w2" else 2 * P
+                width = P if kind == "w2" else PAIR
                 for i in range(2):
-                    for c in range(0, 2 * P, width):
+                    for c in range(0, PAIR, width):
                         if entries_on_partitions:
-                            w, x = operands(kind, a, 2 * P * pair + c, width, HALF * half + P * i, P)
+                            w, x = operands(kind, a, PAIR * pair + c, width, HALF * half + P * i, P)
                             passes.append((bank[:, i, c : c + width], x, w))
                         else:
-                            w, x = operands(kind, a, 2 * P * pair + P * i, P, HALF * half + c, width)
+                            w, x = operands(kind, a, PAIR * pair + P * i, P, HALF * half + c, width)
                             passes.append((bank[:, i, c : c + width], w, x))
             for i, (place, still, moving) in enumerate(passes):
                 nc.tensor.matmul_mx(place, lhsT=still[0], lhsT_scale=still[1], rhs=moving[0], rhs_scale=moving[1],
                                     start=(i == 0), stop=(i == len(passes) - 1))
 
-        inside = [("w3", a) for a in range(KA)] + [("w2", b) for b in range(HA)]
-        beside = [("w4", b) for b in range(HA)]
         for unit, (pair, half) in enumerate(UNITS):
             if unit == 1:
-                finish_half(rest, 1)
-            p2 = psum.tile([P, 2, 2 * P], F32, name="p2", tag="p2", bufs=3)
-            p4 = psum.tile([P, 2, 2 * P], F32, name="p4", tag="p4", bufs=2)
-            products(p2, inside, pair, half, unit > 0)
-            products(p4, beside, pair, half, unit > 0)
-            bounded = ring.tile([P, 2, 2 * P], F32, name="bounded", tag="bounded", align_bytes=64)
-            nc.scalar.activation(bounded[:], p2[:], ACT.Tanh)
-            y = ring.tile([P, 2, HALF], F32, name="y", tag="y_sb")
+                finish_half(second_half, 1, "x_half")
+            inside = psum.tile([P, 2, PAIR], F32, name="inside", tag="inside", bufs=3)
+            beside = psum.tile([P, 2, PAIR], F32, name="beside", tag="beside", bufs=2)
+            terms = [("w3", a) for a in range(K_PASSES)] + [("w2", b) for b in range(R_PASSES)]
+            products(inside, terms, pair, half, unit > 0)
+            products(beside, [("w4", b) for b in range(R_PASSES)], pair, half, unit > 0)
+            bounded = ring.tile([P, 2, PAIR], F32, name="bounded", tag="bounded", align_bytes=MX_ALIGN)
+            nc.scalar.activation(bounded[:], inside[:], ACT.Tanh)
+            y = ring.tile([P, 2, HALF], F32, name="y", tag="y")
             if unit == 0:
-                nc.vector.tensor_tensor(y[:], p4[:], bounded[:], ADD)
+                nc.vector.tensor_tensor(y[:], beside[:], bounded[:], ADD)
             else:
-                bare = ring.tile([P, 2, 2 * P], F32, name="bare", tag="bare")
-                nc.scalar.copy(bare[:], p4[:])
-                y_ps = banks[unit % 2][:].rearrange("p (i t j) -> p i t j", i=2, t=2)
+                bare = ring.tile([P, 2, PAIR], F32, name="bare", tag="bare")
+                nc.scalar.copy(bare[:], beside[:])
+                total = banks[unit % 2][:].rearrange("p (i t j) -> p i t j", i=2, t=2)
                 for i in range(2):
                     for t in range(2):
                         ns = slice(P * i, P * (i + 1))
-                        nc.tensor.matmul(y_ps[:, i, t, :], bounded[:, t, ns], ident[:],
+                        nc.tensor.matmul(total[:, i, t, :], bounded[:, t, ns], ident[:],
                                          start=True, stop=False, is_transpose=True)
-                        nc.tensor.matmul(y_ps[:, i, t, :], bare[:, t, ns], ident[:],
+                        nc.tensor.matmul(total[:, i, t, :], bare[:, t, ns], ident[:],
                                          start=False, stop=True, is_transpose=True)
                 nc.scalar.copy(y[:].rearrange("p i j -> p (i j)"), banks[unit % 2][:])
             js = slice(HALF * half, HALF * (half + 1))

@@ -28,18 +28,19 @@ LAST = SLICES - 1
 J_TILES = S // P
 HALF = S // 2
 PAIR = 2 * P
+W4_BYTES = 4 * PACK * N
 MX_ALIGN = 64
 DMA_ALIGN = 256
 
 UNITS = ((0, 0), (1, 0), (0, 1), (1, 1), (2, 0), (2, 1))
 
 QUEUED_BEHIND = {
-    1: (("w1", 3, 2),), 2: (("w1", 5, 3),), 3: (("dealt", 0),), 4: (("dealt", 1),), 5: (("w4_first",),),
-    6: (("w3",),), 7: (("w2",),), 8: (("scales",), ("w4_rest", 0)), 9: (("w4_rest", 1),), 10: (("w4_rest", 2),),
+    1: (("w1", 3, 2),), 2: (("w1", 5, 3),), 3: (("dealt", 0),), 4: (("dealt", 1),),
+    5: (("w4", 0),), 6: (("w3",),), 7: (("w2",),), 8: (("scales",), ("w4", 1)), 10: (("w4", 2),),
 }
 ROUNDED_BESIDE = {
-    1: ("w1", 3, 2), 2: ("w1", 5, 2), 3: ("w1", 7, 1), 4: ("dealt", 0), 5: ("dealt", 1), 7: ("w4_first",),
-    9: ("w4_rest", 0), 10: ("w4_rest", 1), 11: ("w4_rest", 2),
+    1: (("w1", 3, 2),), 2: (("w1", 5, 2),), 3: (("w1", 7, 1),), 4: (("dealt", 0),), 5: (("dealt", 1),),
+    7: (("w4", 0, 0, 768),), 9: (("w4", 1, 0, 512),), 10: (("w4", 1, 512, 768),), 11: (("w4", 2, 0, 768),),
 }
 CODES_AFTER_TRIAL = {1: "w1_5", 2: "w1_7", 4: "w1_dealt", 5: "x_0", 7: "w4_first"}
 FETCHED_BEHIND = {9: (8,), 10: (9, 10), 11: (11,)}
@@ -55,6 +56,7 @@ def tile_list_mattress_sag_page_kernel(
         lists = ctx.enter_context(tc.tile_pool(name="lists", bufs=1))
         keep = ctx.enter_context(tc.tile_pool(name="keep", bufs=1))
         ring = ctx.enter_context(tc.tile_pool(name="ring", bufs=2))
+        twice = ctx.enter_context(tc.tile_pool(name="twice", bufs=1))
         psum = ctx.enter_context(tc.psum_pool(name="psum", bufs=2))
 
         def load_list(src, name):
@@ -128,7 +130,7 @@ def tile_list_mattress_sag_page_kernel(
         w1_dealt = {}
         w4_rounded = keep.tile([P, R_PASSES, PACK * N], BF16, name="w4_rounded", align_bytes=MX_ALIGN)
         w4_s = keep.tile([P, R_PASSES, N], U8, name="w4_s", align_bytes=MX_ALIGN)
-        w4_first = []
+        w4_w = {}
         waiting = {}
 
         def load_group(kind, *args):
@@ -146,13 +148,14 @@ def tile_list_mattress_sag_page_kernel(
                         w1_raw[(a, s0 + i)] = (rows, P * i)
             elif kind == "dealt":
                 other_raw[(kind, args[0])] = load_rows(raw_tile(PACK * PASS)[:], w1, args[0], P * DEALT, PASS)
-            elif kind == "w4_first":
-                two = raw_tile(2 * PACK * PAIR)
-                one = raw_tile(PACK * PAIR)
-                for b, dst in enumerate((two[:, 0 : PACK * PAIR], two[:, PACK * PAIR : 2 * PACK * PAIR], one[:])):
-                    other_raw[(kind, b)] = load_rows(dst, w4, b, 0, PAIR)
-            elif kind == "w4_rest":
-                other_raw[(kind, args[0])] = load_rows(raw_tile(PACK * (N - PAIR))[:], w4, args[0], PAIR, N - PAIR)
+            elif kind == "w4":
+                b = args[0]
+                if b < 2:
+                    rows = twice.tile([P, PACK * N], F32, name="w4_raw%d" % b, offset=W4_BYTES * (1 - b),
+                                      align_bytes=DMA_ALIGN)
+                else:
+                    rows = ring.tile([P, PACK * N], F32, name="w4_raw", tag="early", bufs=1, align_bytes=DMA_ALIGN)
+                other_raw[(kind, b)] = load_rows(rows[:], w4, b, 0, N)
             elif kind == "w2":
                 nc.sync.dma_start(w2_w[:].bitcast(I32), w2_words.rearrange("a p c -> p a c").bitcast(I32))
             elif kind == "w3":
@@ -192,11 +195,15 @@ def tile_list_mattress_sag_page_kernel(
                     cols = slice(P * i, P * (i + 1))
                     w1_q[(a, DEALT + i)] = (codes[:, a, cols], scales[:, a, cols])
 
+        def quantize_w4(b, codes, c0, c1):
+            quantize(codes, w4_s[:, b, c0:c1], w4_rounded[:, b, PACK * c0 : PACK * c1])
+            for c in range(c0, c1, PAIR):
+                w4_w[(b, c // PAIR)] = codes[:, c - c0 : c - c0 + PAIR]
+
         def quantize_w4_first():
-            codes = keep.tile([P, R_PASSES, PAIR], U32, name="w4_w", tag="w4_first", align_bytes=MX_ALIGN)
-            for b in range(R_PASSES):
-                quantize(codes[:, b, :], w4_s[:, b, 0:PAIR], w4_rounded[:, b, 0 : PACK * PAIR])
-                w4_first.append(codes[:, b, :])
+            codes = keep.tile([P, N], U32, name="w4_w", tag="w4_first", align_bytes=MX_ALIGN)
+            quantize_w4(0, codes[:, 0:PAIR], 0, PAIR)
+            quantize_w4(0, codes[:, PAIR:N], PAIR, N)
 
         waiting["w1_dealt"] = quantize_w1_dealt
         waiting["w4_first"] = quantize_w4_first
@@ -221,16 +228,10 @@ def tile_list_mattress_sag_page_kernel(
                     w1_dealt[a][:].rearrange("p (t m i) -> p m t i", t=PACK, i=PACK),
                     other_raw[(kind, a)].rearrange("p i (m t) -> p m t i", t=PACK),
                 )
-            elif kind == "w4_first":
-                for b in range(R_PASSES):
-                    round_rows(w4_rounded[:, b, 0 : PACK * PAIR], other_raw[(kind, b)])
             else:
-                b = args[0]
-                for c in range(PAIR, N, PAIR):
-                    round_rows(
-                        w4_rounded[:, b, PACK * c : PACK * (c + PAIR)],
-                        other_raw[(kind, b)][:, :, c - PAIR : c],
-                    )
+                b, c0, c1 = args
+                for c in range(c0, c1, PAIR):
+                    round_rows(w4_rounded[:, b, PACK * c : PACK * (c + PAIR)], other_raw[(kind, b)][:, :, c : c + PAIR])
 
         factors = {}
         pages = {}
@@ -309,9 +310,12 @@ def tile_list_mattress_sag_page_kernel(
                 )
 
             def finish():
-                pool = keep if b == 0 else ring
-                x_w[b] = pool.tile([P, S], U32, name="x_w", tag="x_%d" % b, bufs=1, align_bytes=MX_ALIGN)
-                quantize(x_w[b][:], x_s[:, b, :], rounded[:].rearrange("p h w -> p (h w)").bitcast(BF16))
+                pool, extra = (keep, 0) if b == 0 else (ring, PAIR)
+                codes = pool.tile([P, S + extra], U32, name="x_w", tag="x_%d" % b, bufs=1, align_bytes=MX_ALIGN)
+                x_w[b] = codes[:, 0:S]
+                quantize(x_w[b], x_s[:, b, :], rounded[:].rearrange("p h w -> p (h w)").bitcast(BF16))
+                if extra:
+                    quantize_w4(1, codes[:, S : S + extra], 0, PAIR)
 
             waiting["x_%d" % b] = finish
 
@@ -366,7 +370,8 @@ def tile_list_mattress_sag_page_kernel(
                 early = ring.tile([P, K_PASSES, PACK * 2 * P], F32, name="early", tag="early", bufs=1,
                                   align_bytes=DMA_ALIGN)
                 rows = [load_rows(early[:, a, :], w1, a, P, 2 * P) for a in range(K_PASSES)]
-                round_w1(1, 2, rows, "fetched", 1)()
+                round_w1(1, 1, [r[:, :, 0:P] for r in rows], "fetched", 1)()
+                round_w1(2, 1, [r[:, :, P : 2 * P] for r in rows], "w1_rounded", 2)()
                 fetched = ring.tile([P, S], F32, name="fetched", tag="fetched", bufs=1, align_bytes=MX_ALIGN)
             if 2 <= s < DEALT + 2:
                 turn(s - 2, banks[s % 2])
@@ -383,13 +388,13 @@ def tile_list_mattress_sag_page_kernel(
                 nc.sync.dma_start(gain_dealt[:], gain[P * DEALT : H].rearrange("(p i) -> p i", i=PACK))
             for group in QUEUED_BEHIND.get(s, ()):
                 load_group(*group)
-            if s in ROUNDED_BESIDE:
-                round_group(*ROUNDED_BESIDE[s])
+            for group in ROUNDED_BESIDE.get(s, ()):
+                round_group(*group)
             if s - 2 in CODES_AFTER_TRIAL:
                 waiting[CODES_AFTER_TRIAL[s - 2]]()
             if s > PACK and s % PACK == 1:
                 turn_back(s // PACK - 1)
-            if s == PACK + 1:
+            if s == 6:
                 deal_factors()
 
         finish_half(first_half, 0, "w4_late")
@@ -397,18 +402,18 @@ def tile_list_mattress_sag_page_kernel(
                                 align_bytes=MX_ALIGN)
         for s in range(DEALT, SLICES):
             fetch_dealt(s, second_half, 1)
-        w4_early = ring.tile([P, N - PAIR], U32, name="w4_early", tag="w4_early", bufs=1, align_bytes=MX_ALIGN)
+        w4_early = ring.tile([P, PAIR], U32, name="w4_early", tag="w4_early", bufs=1, align_bytes=MX_ALIGN)
         w4_late = ring.tile([P, 2, N - PAIR], U32, name="w4_late", tag="w4_late", bufs=1, align_bytes=MX_ALIGN)
-        w4_rest = [w4_early[:], w4_late[:, 0, :], w4_late[:, 1, :]]
-        for b in range(R_PASSES):
-            quantize(w4_rest[b], w4_s[:, b, PAIR:N], w4_rounded[:, b, PACK * PAIR : PACK * N])
+        quantize_w4(2, w4_early[:], 0, PAIR)
+        for b in (1, 2):
+            quantize_w4(b, w4_late[:, b - 1, :], PAIR, N)
 
         idx4 = load_list(offs4, "idx4")
         wgo_sb = keep.tile([P, S], F32, name="wgo_sb")
         nc.sync.dma_start(wgo_sb[:], wgo)
         out_pages = []
         for n in range(N // P):
-            out_page = keep.tile([P, T2], F32, name="out_page%d" % n, align_bytes=DMA_ALIGN)
+            out_page = twice.tile([P, T2], F32, name="out_page%d" % n, offset=4 * T2 * n, align_bytes=DMA_ALIGN)
             nc.sync.dma_start(out_page[:], page1[P * n : P * (n + 1), :])
             out_pages.append(out_page)
 
@@ -420,7 +425,7 @@ def tile_list_mattress_sag_page_kernel(
             x = (x_w[a][:, js].bitcast(FP8X4), x_s[:, a, js])
             if kind == "w2":
                 return (w2_w[:, a, 2 * n0 : 2 * (n0 + n_width)].bitcast(FP4X4), w2_s[:, a, ns]), x
-            codes = w4_first[a][:, ns] if n0 < PAIR else w4_rest[a][:, n0 - PAIR : n0 - PAIR + n_width]
+            codes = w4_w[(a, n0 // PAIR)][:, n0 % PAIR : n0 % PAIR + n_width]
             return (codes.bitcast(FP8X4), w4_s[:, a, ns]), x
 
         def products(bank, terms, pair, half, entries_on_partitions):

from contextlib import ExitStack

import concourse.mybir as mybir
from concourse.masks import make_identity

K, H, N, T, S, T2 = 1024, 1536, 768, 2048, 512, 1024
FLOPS = 2 * S * (K * H + H * N + K * N + H * N)

F32 = mybir.dt.float32
BF16 = mybir.dt.bfloat16
I32 = mybir.dt.int32
U32 = mybir.dt.uint32
U16 = mybir.dt.uint16
U8 = mybir.dt.uint8
FP8X4 = mybir.dt.float8_e4m3fn_x4
FP4X4 = mybir.dt.float4_e2m1fn_x4
ACT = mybir.ActivationFunctionType
MULT = mybir.AluOpType.mult
ADD = mybir.AluOpType.add

P = 128
PACK = 4
PASS = P * PACK
K_PASSES, R_PASSES = K // PASS, H // PASS
SLICES = H // P
DEALT = SLICES - PACK
LAST = SLICES - 1
J_TILES = S // P
HALF = S // 2
PAIR = 2 * P
W4_BYTES = 4 * PACK * N
MX_ALIGN = 64
DMA_ALIGN = 256

UNITS = ((0, 0), (1, 0), (0, 1), (1, 1), (2, 0), (2, 1))

QUEUED_BEHIND = {
    1: (("w1", 3, 2),), 2: (("w1", 5, 3),), 3: (("dealt", 0),), 4: (("dealt", 1),),
    5: (("w4", 0),), 6: (("w3",),), 7: (("w2",),), 8: (("scales",), ("w4", 1)), 10: (("w4", 2),),
}
ROUNDED_BESIDE = {
    1: (("w1", 3, 2),), 2: (("w1", 5, 2),), 3: (("w1", 7, 1),), 4: (("dealt", 0),), 5: (("dealt", 1),),
    7: (("w4", 0, 0, 768),), 9: (("w4", 1, 0, 512),), 10: (("w4", 1, 512, 768),), 11: (("w4", 2, 0, 768),),
}
CODES_AFTER_TRIAL = {1: "w1_5", 2: "w1_7", 4: "w1_dealt", 5: "x_0", 7: "w4_first"}
FETCHED_BEHIND = {9: (8,), 10: (9, 10), 11: (11,)}
H_TAGS = {LAST - 1: "x_1", LAST: "second_half"}


def tile_list_mattress_sag_page_kernel(
    tc, tab_words, tab_scales, offs, w1, gain, page0, offs2, wgs, offs3, trial,
    w2_words, w2_scales, w3_words, w3_scales, w4, page1, offs4, wgo, out,
):
    nc = tc.nc
    with ExitStack() as ctx:
        lists = ctx.enter_context(tc.tile_pool(name="lists", bufs=1))
        keep = ctx.enter_context(tc.tile_pool(name="keep", bufs=1))
        ring = ctx.enter_context(tc.tile_pool(name="ring", bufs=2))
        twice = ctx.enter_context(tc.tile_pool(name="twice", bufs=1))
        psum = ctx.enter_context(tc.psum_pool(name="psum", bufs=2))

        def load_list(src, name):
            entries = lists.tile([P, S // 16], U16, name=name)
            nc.sync.dma_start(entries[:], src)
            return entries

        def raw_tile(columns, dtype=F32):
            return ring.tile([P, columns], dtype, name="raw", tag="raw", bufs=4, align_bytes=DMA_ALIGN)

        def load_rows(dst, src, a, c0, width):
            rows = dst.rearrange("p (i c) -> p i c", i=PACK)
            block = src[PASS * a : PASS * (a + 1), c0 : c0 + width]
            nc.sync.dma_start(rows, block.rearrange("(p i) c -> p i c", i=PACK))
            return rows

        def round_rows(dst, rows):
            nc.scalar.copy(
                dst.rearrange("p (c e i) -> p c i e", e=4, i=PACK),
                rows.rearrange("p i (c e) -> p c i e", e=4),
            )

        def quantize(codes, scales, rounded):
            nc.vector.quantize_mx(codes.bitcast(FP8X4), scales, rounded)

        def dealt_rows(src, s):
            return src[P * DEALT : H, :].rearrange("(p i) c -> p i c", i=PACK)[:, s - DEALT, :]

        idx = load_list(offs, "idx")
        tab_s = keep.tile([P, T], U8, name="tab_s", align_bytes=MX_ALIGN)
        nc.gpsimd.memset(tab_s[:].bitcast(I32), 0)
        gain_rows = keep.tile([P, P], F32, name="gain_rows")
        nc.vector.memset(gain_rows[:], 0.0)
        zeros = keep.tile([P, 1], F32, name="zeros")
        nc.vector.memset(zeros[:], 0.0)
        no_bias = keep.tile([P, 1], F32, name="no_bias")
        nc.scalar.activation(no_bias[:], zeros[:], ACT.Silu)
        v_w = []
        v_s = keep.tile([P, S], U8, name="v_s", align_bytes=MX_ALIGN)
        for a in range(K_PASSES):
            tab_w = raw_tile(T, U32)
            nc.sync.dma_start(tab_w[:].bitcast(I32), tab_words[a].rearrange("p t i -> p (t i)").bitcast(I32))
            picked_w = keep.tile([P, S], U32, name="v_w%d" % a, align_bytes=MX_ALIGN)
            nc.vector.tensor_copy(picked_w[:], tab_w[:].indirect(idx[:]))
            v_w.append(picked_w)
            if a == 0:
                for q in range(4):
                    nc.sync.dma_start(
                        tab_s[32 * q : 32 * q + 4 * K_PASSES, :].bitcast(I32),
                        tab_scales[:, 4 * q : 4 * q + 4, :].bitcast(I32),
                    )
                nc.sync.dma_start(gain_rows[0:DEALT, :], gain[0 : P * DEALT].rearrange("(s q) -> s q", q=P))
                nc.vector.tensor_copy(v_s[:], tab_s[:].indirect(idx[:]))

        ident = keep.tile([P, P], F32, name="ident")
        make_identity(nc, ident[:])
        w2_s = keep.tile([P, R_PASSES, N], U8, name="w2_s", align_bytes=MX_ALIGN)
        w3_s = keep.tile([P, K_PASSES, N], U8, name="w3_s", align_bytes=MX_ALIGN)
        nc.gpsimd.memset(w2_s[:].rearrange("p a c -> p (a c)").bitcast(I32), 0)
        nc.gpsimd.memset(w3_s[:].rearrange("p a c -> p (a c)").bitcast(I32), 0)

        banks = [psum.tile([P, S], F32, name="bank%d" % i, bufs=1) for i in range(2)]
        gain_turned = psum.tile([P, P], F32, name="gain_turned", tag="turn", bufs=1)
        nc.tensor.transpose(gain_turned[:], gain_rows[:], ident[:])
        gain_plain = keep.tile([P, DEALT], F32, name="gain_plain")
        nc.scalar.copy(gain_plain[:], gain_turned[:, 0:DEALT])

        w1_q = {}
        w1_raw = {}
        other_raw = {}
        w1_dealt = {}
        w4_rounded = keep.tile([P, R_PASSES, PACK * N], BF16, name="w4_rounded", align_bytes=MX_ALIGN)
        w4_s = keep.tile([P, R_PASSES, N], U8, name="w4_s", align_bytes=MX_ALIGN)
        w4_w = {}
        waiting = {}

        def load_group(kind, *args):
            if kind == "w1":
                s0, count = args
                width = P * count
                shared = raw_tile(K_PASSES * PACK * width) if K_PASSES * width <= PASS else None
                for a in range(K_PASSES):
                    if shared is None:
                        dst = raw_tile(PACK * width)[:]
                    else:
                        dst = shared[:, PACK * width * a : PACK * width * (a + 1)]
                    rows = load_rows(dst, w1, a, P * s0, width)
                    for i in range(count):
                        w1_raw[(a, s0 + i)] = (rows, P * i)
            elif kind == "dealt":
                other_raw[(kind, args[0])] = load_rows(raw_tile(PACK * PASS)[:], w1, args[0], P * DEALT, PASS)
            elif kind == "w4":
                b = args[0]
                if b < 2:
                    rows = twice.tile([P, PACK * N], F32, name="w4_raw%d" % b, offset=W4_BYTES * (1 - b),
                                      align_bytes=DMA_ALIGN)
                else:
                    rows = ring.tile([P, PACK * N], F32, name="w4_raw", tag="early", bufs=1, align_bytes=DMA_ALIGN)
                other_raw[(kind, b)] = load_rows(rows[:], w4, b, 0, N)
            elif kind == "w2":
                nc.sync.dma_start(w2_w[:].bitcast(I32), w2_words.rearrange("a p c -> p a c").bitcast(I32))
            elif kind == "w3":
                nc.sync.dma_start(w3_w[:].bitcast(I32), w3_words.rearrange("a p c i -> p a (c i)").bitcast(I32))
            else:
                for q in range(4):
                    for dst, src in ((w2_s, w2_scales), (w3_s, w3_scales)):
                        nc.sync.dma_start(
                            dst[32 * q : 32 * q + 4, :, :].bitcast(I32),
                            src[:, 4 * q : 4 * q + 4, :].rearrange("a r c -> r a c").bitcast(I32),
                        )

        def round_w1(s0, count, rows, tag, bufs):
            width = P * count
            rounded = ring.tile([P, K_PASSES, PACK * width], BF16, name="w1_rounded", tag=tag, bufs=bufs,
                                align_bytes=MX_ALIGN)
            for a in range(K_PASSES):
                round_rows(rounded[:, a, :], rows[a])

            def finish():
                codes = keep.tile([P, K_PASSES, width], U32, name="w1_w", tag="w1_%d" % s0, align_bytes=MX_ALIGN)
                scales = keep.tile([P, K_PASSES, width], U8, name="w1_s%d" % s0, align_bytes=MX_ALIGN)
                quantize(*(t[:].rearrange("p a c -> p (a c)") for t in (codes, scales, rounded)))
                for a in range(K_PASSES):
                    for i in range(count):
                        cols = slice(P * i, P * (i + 1))
                        w1_q[(a, s0 + i)] = (codes[:, a, cols], scales[:, a, cols])

            return finish

        def quantize_w1_dealt():
            codes = keep.tile([P, K_PASSES, PASS], U32, name="w1_w", tag="w1_dealt", align_bytes=MX_ALIGN)
            scales = keep.tile([P, K_PASSES, PASS], U8, name="w1_s_dealt", align_bytes=MX_ALIGN)
            for a in range(K_PASSES):
                quantize(codes[:, a, :], scales[:, a, :], w1_dealt[a][:])
                for i in range(PACK):
                    cols = slice(P * i, P * (i + 1))
                    w1_q[(a, DEALT + i)] = (codes[:, a, cols], scales[:, a, cols])

        def quantize_w4(b, codes, c0, c1):
            quantize(codes, w4_s[:, b, c0:c1], w4_rounded[:, b, PACK * c0 : PACK * c1])
            for c in range(c0, c1, PAIR):
                w4_w[(b, c // PAIR)] = codes[:, c - c0 : c - c0 + PAIR]

        def quantize_w4_first():
            codes = keep.tile([P, N], U32, name="w4_w", tag="w4_first", align_bytes=MX_ALIGN)
            quantize_w4(0, codes[:, 0:PAIR], 0, PAIR)
            quantize_w4(0, codes[:, PAIR:N], PAIR, N)

        waiting["w1_dealt"] = quantize_w1_dealt
        waiting["w4_first"] = quantize_w4_first

        def round_group(kind, *args):
            if kind == "w1":
                s0, count = args
                rows = []
                for a in range(K_PASSES):
                    loaded, c0 = w1_raw[(a, s0)]
                    rows.append(loaded[:, :, c0 : c0 + P * count])
                finish = round_w1(s0, count, rows, "w1_rounded", 2)
                if "w1_%d" % s0 in CODES_AFTER_TRIAL.values():
                    waiting["w1_%d" % s0] = finish
                else:
                    finish()
            elif kind == "dealt":
                a = args[0]
                w1_dealt[a] = ring.tile([P, PACK * PASS], BF16, name="w1_rounded", tag="w1_rounded", bufs=2,
                                        align_bytes=MX_ALIGN)
                nc.scalar.copy(
                    w1_dealt[a][:].rearrange("p (t m i) -> p m t i", t=PACK, i=PACK),
                    other_raw[(kind, a)].rearrange("p i (m t) -> p m t i", t=PACK),
                )
            else:
                b, c0, c1 = args
                for c in range(c0, c1, PAIR):
                    round_rows(w4_rounded[:, b, PACK * c : PACK * (c + PAIR)], other_raw[(kind, b)][:, :, c : c + PAIR])

        factors = {}
        pages = {}

        def deal_factors():
            turned = psum.tile([P, J_TILES, P], F32, name="turned", tag="turn", bufs=1)
            for jt in range(J_TILES):
                nc.tensor.transpose(turned[:, jt, :], wgs_sb[:, P * jt : P * (jt + 1)], ident[:])
            three = keep.tile([P, PACK - 1, S], F32, name="factors_dealt")
            fourth = ring.tile([P, S], F32, name="factors_last", tag="w4_early", bufs=1, align_bytes=MX_ALIGN)
            for i in range(PACK):
                repeated = keep.tile([P, J_TILES, 4, 32], F32, name="repeated")
                every_fourth = turned[:].rearrange("j a (p i) -> j i a p", i=PACK)[:, i, :, :]
                nc.scalar.copy(repeated[:], every_fourth.unsqueeze(2).to_broadcast([P, J_TILES, 4, 32]))
                rows = psum.tile([P, J_TILES, P], F32, name="rows", tag="inside", bufs=3)
                for jt in range(J_TILES):
                    nc.tensor.transpose(rows[:, jt, :], repeated[:, jt, :, :].rearrange("j r p -> j (r p)"), ident[:])
                factors[DEALT + i] = three[:, i, :] if i < PACK - 1 else fourth[:]
                nc.scalar.activation(
                    factors[DEALT + i], rows[:].rearrange("p a j -> p (a j)"), ACT.Copy, scale=gain_dealt[:, i : i + 1]
                )

        def put_slice(s):
            product = banks[s % 2]
            if s < DEALT:
                nc.scalar.activation(factors[s], wgs_sb[:], ACT.Copy, scale=gain_plain[:, s : s + 1])
            for a in range(K_PASSES):
                codes, scales = w1_q[(a, s)]
                nc.tensor.matmul_mx(
                    product[:], lhsT=codes.bitcast(FP8X4), lhsT_scale=scales,
                    rhs=v_w[a][:].bitcast(FP8X4), rhs_scale=v_s[4 * a : P, :],
                    start=(a == 0), stop=(a == K_PASSES - 1),
                )
            h = ring.tile([P, S], F32, name="h", tag=H_TAGS.get(s, "h"), bufs=1 if s in H_TAGS else 2,
                          align_bytes=MX_ALIGN)
            nc.scalar.activation(h[:], product[:], ACT.Silu, bias=no_bias[:] if s == 0 else 0.0)
            page = ring.tile([P, T2], F32, name="page", tag="page", bufs=5, align_bytes=DMA_ALIGN)
            nc.sync.dma_start(page[:], page0[P * s : P * (s + 1), :] if s < DEALT else dealt_rows(page0, s))
            nc.vector.tensor_tensor(page[:].indirect(idx2[:]), h[:], factors[s], MULT)
            pages[s] = page

        x_turned = {}
        x_w = {}
        x_s = keep.tile([P, R_PASSES, S], U8, name="x_s", align_bytes=MX_ALIGN)

        def turn(s, bank):
            b, quarter = divmod(s, PACK)
            if s in CODES_AFTER_TRIAL:
                given = keep.tile([P, S], F32, name="given", tag=CODES_AFTER_TRIAL[s], align_bytes=MX_ALIGN)
            else:
                given = ring.tile([P, S], F32, name="given", tag="given", bufs=1)
            nc.sync.dma_start(given[:], trial[P * s : P * (s + 1), :])
            for i, src in enumerate((given, fetched)):
                for c in range(0, S, P):
                    nc.tensor.matmul(bank[:, c : c + P], src[:, c : c + P], ident[:],
                                     start=(i == 0 and c == 0), stop=(i == 1 and c == S - P), is_transpose=True)
            if quarter == 0:
                x_turned[b] = ring.tile([P, J_TILES, 2, P, 2], BF16, name="x_turned", tag="x_turned", bufs=1)
            nc.scalar.copy(
                x_turned[b][:, :, :, 32 * quarter : 32 * (quarter + 1), :],
                bank[:].rearrange("j (t p u e) -> j t u p e", p=32, u=2, e=2),
            )

        def turn_back(b):
            words = x_turned[b][:].rearrange("j t u p e -> j (t u p e)").bitcast(F32)
            rounded = ring.tile([P, 2, S], F32, name="x_rounded", tag="x_rounded", bufs=1, align_bytes=MX_ALIGN)
            for half in range(2):
                back = psum.tile([P, 2, 2, P], F32, name="back", tag="turn", bufs=1)
                for t in range(2):
                    for u in range(2):
                        w0 = P * (2 * (2 * half + t) + u)
                        nc.tensor.transpose(back[:, t, u, :], words[:, w0 : w0 + P], ident[:])
                nc.scalar.copy(
                    rounded[:, half, :].rearrange("p (t j u) -> p t j u", t=2, u=2),
                    back[:].rearrange("p t u j -> p t j u"),
                )

            def finish():
                pool, extra = (keep, 0) if b == 0 else (ring, PAIR)
                codes = pool.tile([P, S + extra], U32, name="x_w", tag="x_%d" % b, bufs=1, align_bytes=MX_ALIGN)
                x_w[b] = codes[:, 0:S]
                quantize(x_w[b], x_s[:, b, :], rounded[:].rearrange("p h w -> p (h w)").bitcast(BF16))
                if extra:
                    quantize_w4(1, codes[:, S : S + extra], 0, PAIR)

            waiting["x_%d" % b] = finish

        given_dealt = {}

        def fetch_dealt(s, dst, half):
            entries = idx3[:, HALF * half // 16 : HALF * (half + 1) // 16]
            nc.vector.tensor_tensor(
                dst[:, s - DEALT, :], pages[s][:].indirect(entries),
                given_dealt[s][:, HALF * half : HALF * (half + 1)], ADD,
            )

        def finish_half(summed, half, tag):
            b = R_PASSES - 1
            rounded = ring.tile([P, PACK * HALF], BF16, name="x_half", tag=tag, bufs=1, align_bytes=MX_ALIGN)
            round_rows(rounded[:], summed[:])
            js = slice(HALF * half, HALF * (half + 1))
            if half == 0:
                x_w[b] = keep.tile([P, S], U32, name="x_w", tag="x_%d" % b, align_bytes=MX_ALIGN)
            quantize(x_w[b][:, js], x_s[:, b, js], rounded[:])

        for a in range(K_PASSES):
            raw = ring.tile([P, PACK * P], F32, name="raw_first", tag="bounded", align_bytes=MX_ALIGN)
            rows = load_rows(raw[:], w1, a, 0, P)
            rounded = keep.tile([P, PACK * P], BF16, name="w1_first%d" % a, align_bytes=MX_ALIGN)
            if a == 0:
                round_rows(rounded[:], rows)
            else:
                nc.vector.tensor_copy(
                    rounded[:].rearrange("p (c i) -> p c i", i=PACK), rows.rearrange("p i c -> p c i")
                )
            codes = keep.tile([P, P], U32, name="w1_w_first%d" % a, align_bytes=MX_ALIGN)
            scales = keep.tile([P, P], U8, name="w1_s_first%d" % a, align_bytes=MX_ALIGN)
            quantize(codes[:], scales[:], rounded[:])
            w1_q[(a, 0)] = (codes[:], scales[:])
        wgs_sb = keep.tile([P, S], F32, name="wgs_sb")
        nc.sync.dma_start(wgs_sb[:], wgs)
        idx2 = load_list(offs2, "idx2")
        idx3 = load_list(offs3, "idx3")
        w2_w = keep.tile([P, R_PASSES, 2 * N], U8, name="w2_w", align_bytes=MX_ALIGN)
        w3_w = keep.tile([P, K_PASSES, N], U32, name="w3_w", align_bytes=MX_ALIGN)
        first_half = keep.tile([P, PACK, HALF], F32, name="first_half")
        for s in range(SLICES):
            if s < 2:
                factors[s] = ring.tile([P, S], F32, name="factors", tag="bare")[:]
            if s == 2:
                later = ring.tile([P, DEALT - 2, S], F32, name="factors", tag="early", bufs=1, align_bytes=DMA_ALIGN)
                for r in range(2, DEALT):
                    factors[r] = later[:, r - 2, :]
            put_slice(s)
            if s == 0:
                early = ring.tile([P, K_PASSES, PACK * 2 * P], F32, name="early", tag="early", bufs=1,
                                  align_bytes=DMA_ALIGN)
                rows = [load_rows(early[:, a, :], w1, a, P, 2 * P) for a in range(K_PASSES)]
                round_w1(1, 1, [r[:, :, 0:P] for r in rows], "fetched", 1)()
                round_w1(2, 1, [r[:, :, P : 2 * P] for r in rows], "w1_rounded", 2)()
                fetched = ring.tile([P, S], F32, name="fetched", tag="fetched", bufs=1, align_bytes=MX_ALIGN)
            if 2 <= s < DEALT + 2:
                turn(s - 2, banks[s % 2])
            if 1 <= s <= DEALT:
                nc.vector.tensor_copy(fetched[:], pages[s - 1][:].indirect(idx3[:]))
            for r in FETCHED_BEHIND.get(s, ()):
                given_dealt[r] = ring.tile([P, S], F32, name="given_dealt", tag="given_dealt", bufs=PACK)
                nc.sync.dma_start(given_dealt[r][:], dealt_rows(trial, r))
                fetch_dealt(r, first_half, 0)
            if H_TAGS.get(s) in waiting:
                waiting[H_TAGS[s]]()
            if s == PACK + 1:
                gain_dealt = keep.tile([P, PACK], F32, name="gain_dealt")
                nc.sync.dma_start(gain_dealt[:], gain[P * DEALT : H].rearrange("(p i) -> p i", i=PACK))
            for group in QUEUED_BEHIND.get(s, ()):
                load_group(*group)
            for group in ROUNDED_BESIDE.get(s, ()):
                round_group(*group)
            if s - 2 in CODES_AFTER_TRIAL:
                waiting[CODES_AFTER_TRIAL[s - 2]]()
            if s > PACK and s % PACK == 1:
                turn_back(s // PACK - 1)
            if s == 6:
                deal_factors()

        finish_half(first_half, 0, "w4_late")
        second_half = ring.tile([P, PACK, HALF], F32, name="second_half", tag="second_half", bufs=1,
                                align_bytes=MX_ALIGN)
        for s in range(DEALT, SLICES):
            fetch_dealt(s, second_half, 1)
        w4_early = ring.tile([P, PAIR], U32, name="w4_early", tag="w4_early", bufs=1, align_bytes=MX_ALIGN)
        w4_late = ring.tile([P, 2, N - PAIR], U32, name="w4_late", tag="w4_late", bufs=1, align_bytes=MX_ALIGN)
        quantize_w4(2, w4_early[:], 0, PAIR)
        for b in (1, 2):
            quantize_w4(b, w4_late[:, b - 1, :], PAIR, N)

        idx4 = load_list(offs4, "idx4")
        wgo_sb = keep.tile([P, S], F32, name="wgo_sb")
        nc.sync.dma_start(wgo_sb[:], wgo)
        out_pages = []
        for n in range(N // P):
            out_page = twice.tile([P, T2], F32, name="out_page%d" % n, offset=4 * T2 * n, align_bytes=DMA_ALIGN)
            nc.sync.dma_start(out_page[:], page1[P * n : P * (n + 1), :])
            out_pages.append(out_page)

        def operands(kind, a, n0, n_width, j0, j_width):
            ns = slice(n0, n0 + n_width)
            js = slice(j0, j0 + j_width)
            if kind == "w3":
                return (w3_w[:, a, ns].bitcast(FP8X4), w3_s[:, a, ns]), (v_w[a][:, js].bitcast(FP8X4), v_s[4 * a : P, js])
            x = (x_w[a][:, js].bitcast(FP8X4), x_s[:, a, js])
            if kind == "w2":
                return (w2_w[:, a, 2 * n0 : 2 * (n0 + n_width)].bitcast(FP4X4), w2_s[:, a, ns]), x
            codes = w4_w[(a, n0 // PAIR)][:, n0 % PAIR : n0 % PAIR + n_width]
            return (codes.bitcast(FP8X4), w4_s[:, a, ns]), x

        def products(bank, terms, pair, half, entries_on_partitions):
            passes = []
            for kind, a in terms:
                width = P if kind == "w2" else PAIR
                for i in range(2):
                    for c in range(0, PAIR, width):
                        if entries_on_partitions:
                            w, x = operands(kind, a, PAIR * pair + c, width, HALF * half + P * i, P)
                            passes.append((bank[:, i, c : c + width], x, w))
                        else:
                            w, x = operands(kind, a, PAIR * pair + P * i, P, HALF * half + c, width)
                            passes.append((bank[:, i, c : c + width], w, x))
            for i, (place, still, moving) in enumerate(passes):
                nc.tensor.matmul_mx(place, lhsT=still[0], lhsT_scale=still[1], rhs=moving[0], rhs_scale=moving[1],
                                    start=(i == 0), stop=(i == len(passes) - 1))

        for unit, (pair, half) in enumerate(UNITS):
            if unit == 1:
                finish_half(second_half, 1, "x_half")
            inside = psum.tile([P, 2, PAIR], F32, name="inside", tag="inside", bufs=3)
            beside = psum.tile([P, 2, PAIR], F32, name="beside", tag="beside", bufs=2)
            terms = [("w3", a) for a in range(K_PASSES)] + [("w2", b) for b in range(R_PASSES)]
            products(inside, terms, pair, half, unit > 0)
            products(beside, [("w4", b) for b in range(R_PASSES)], pair, half, unit > 0)
            bounded = ring.tile([P, 2, PAIR], F32, name="bounded", tag="bounded", align_bytes=MX_ALIGN)
            nc.scalar.activation(bounded[:], inside[:], ACT.Tanh)
            y = ring.tile([P, 2, HALF], F32, name="y", tag="y")
            if unit == 0:
                nc.vector.tensor_tensor(y[:], beside[:], bounded[:], ADD)
            else:
                bare = ring.tile([P, 2, PAIR], F32, name="bare", tag="bare")
                nc.scalar.copy(bare[:], beside[:])
                total = banks[unit % 2][:].rearrange("p (i t j) -> p i t j", i=2, t=2)
                for i in range(2):
                    for t in range(2):
                        ns = slice(P * i, P * (i + 1))
                        nc.tensor.matmul(total[:, i, t, :], bounded[:, t, ns], ident[:],
                                         start=True, stop=False, is_transpose=True)
                        nc.tensor.matmul(total[:, i, t, :], bare[:, t, ns], ident[:],
                                         start=False, stop=True, is_transpose=True)
                nc.scalar.copy(y[:].rearrange("p i j -> p (i j)"), banks[unit % 2][:])
            js = slice(HALF * half, HALF * (half + 1))
            entries = idx4[:, HALF * half // 16 : HALF * (half + 1) // 16]
            for i in range(2):
                n = 2 * pair + i
                nc.vector.tensor_tensor(out_pages[n][:].indirect(entries), y[:, i, :], wgo_sb[:, js], MULT)
                if half == 1:
                    nc.sync.dma_start(out[P * n : P * (n + 1), :], out_pages[n][:])
